import numpy as np, ml_dtypes
CORES = [83,85,87,115,117,119]
N = 6
BF = ml_dtypes.bfloat16
W, K, T, S, ND = 4096, 384, 3, 5, 2
def stir(rng, a, n):
    r = rng.random(a.shape, dtype=np.float32)
    s = np.concatenate([np.sort(r, axis=-1), np.full(r.shape[:-1] + (1,), 2, np.float32)], axis=-1)
    return np.where(r < np.take_along_axis(s, n[..., None], -1), (a + rng.integers(1, 64, a.shape)) & 63, a)
def near(rng, pro, n, counts):
    a = pro[np.arange(8)[None, :, None], rng.integers(0, pro.shape[1], (N, 8, n))]
    return stir(rng, a, rng.choice(np.array(counts), (N, 8, n)))
def protos(rng, first):
    return stir(rng, np.repeat(first, 2, axis=1), np.full((8, 2), 3))
def parts(rng):
    pro = protos(rng, rng.integers(0, 64, (8, 1, 16)))
    return (near(rng, pro, K, [0, 1, 1, 2, 2, 3, 16]), rng.integers(0, 256, (N, 8, K, 16)), near(rng, pro, W, [0, 1, 1, 2, 3, 16]), rng.integers(0, 256, (N, 8, W, 16)),
            rng.integers(0, 256, (8, 16, 2)), rng.integers(900, 1900, (N, 8, 16)))
def tile(a):
    return np.ascontiguousarray(a.transpose(0, 1, 3, 2)).reshape(N, 128, -1).astype(np.float32).astype(BF)
def pack(x, g, lx, lm, w, lim):
    return {"xw": tile(x), "gw": tile(g), "lex": tile(lx), "mng": tile(lm),
            "wts": np.ascontiguousarray(np.broadcast_to(w.reshape(1, 128, 2), (N, 128, 2))).astype(np.int32), "th": lim.reshape(N, 128, 1).astype(np.int32)}
def setup_inputs(rng):
    return pack(*parts(rng))
def setup_inputs_spread(rng):
    pro = protos(rng, (64 * rng.random((8, 1, 16)) ** 3).astype(np.int64))
    x = near(rng, pro, K, [0, 1, 1, 2, 3, 4, 16]); lx = near(rng, pro, W, [0, 1, 1, 2, 4, 16])
    g = np.floor(256 * rng.random((N, 8, K, 1)) ** 2 * rng.random((N, 8, K, 16))).astype(np.int64)
    lm = np.floor(256 * rng.random((N, 8, W, 1)) ** 2 * rng.random((N, 8, W, 16))).astype(np.int64)
    w = np.exp2(8 * rng.random((8, 16, 2))).astype(np.int64) - 1; w = np.where(rng.random(w.shape) < 0.25, rng.integers(0, 256, w.shape), w)
    lim = np.minimum(np.exp2(4 + 8.2 * rng.random((N, 8, 16))).astype(np.int64), 4081)
    return pack(x, g, lx, lm, w, lim)
def setup_inputs_ends(rng):
    base = np.repeat(63 * rng.integers(0, 2, (8, 1, 16)), 2, axis=1); base[:, 1] = np.where(rng.random((8, 16)) < 0.15, 63 - base[:, 1], base[:, 1])
    def some(n, share):
        a = base[np.arange(8)[None, :, None], rng.integers(0, 2, (N, 8, n))]
        return np.where(rng.random(a.shape) < share, np.where(rng.random(a.shape) < 0.6, 63 - a, rng.choice(np.array([1, 31, 62]), a.shape)), a)
    def both(n):
        return 255 * np.where(rng.random((N, 8, n, 1)) < 0.5, rng.integers(0, 2, (N, 8, n, 1)), rng.integers(0, 2, (N, 8, n, 16)))
    x = some(K, 0.08); lx = some(W, 0.1); g = both(K); lm = both(W)
    w = 255 * rng.integers(0, 2, (8, 16, 2)); w[:5, 15] = 65; w[5, :, 0] = 255; w[6, 0] = 65; w[7, 14:, 0] = 65; w[7, 14:, 1] = 0
    w[4, 13, 0] = 89; w[4, 13, 1] = 0; w[4, 14, 0] = 0; w[4, 14, 1] = 227
    lim = np.full((N, 8, 16), 4081); odd = np.arange(N) % 2 == 1
    lim = np.where(odd[:, None, None] & (rng.random(lim.shape) < 0.25), 0, lim); lim[:, 0, 0] = 0
    x[:, 0, :, 0] = 63; lx[:, 0, :, 0] = 63
    x[:, 5, 1] = 63; x[:, 5, K - 1] = 63
    for i in (3, K - 2):
        x[:, 1:5, i] = 0; x[:, 1:5, i, 15] = 63
    p = (((W - 1) ** 2 >> 5) + W - 1) & (W - 1)
    lx[:, 1:5, p] = 0; lx[:, 1:5, p, 15] = 63; lx[:, 1:5, p, 13] = 63
    x[:, 4, 4] = 0; x[:, 4, 4, 13] = 46; x[:, 4, 4, 14] = 36; x[:, 4, 4, 15] = 63
    p = ((4093 * 4075 >> 5) + 4093) & (W - 1)
    lx[:, 4, p] = x[:, 4, 4]; lx[:, 4, p, 0] = 63; lx[:, 4, p + 1] = 63; lm[:, 4, p] = 255; g[:, 4, 4] = 0
    x[:, 7, 4] = 0; x[:, 7, 4, 14] = 63; g[:, 7, 4] = 0
    for i in (5, K - 1):
        x[:, 7, i] = 0; x[:, 7, i, 15] = 63; g[:, 7, i] = 255 if i == 5 else 0
    lx[:, 7, 0] = 63; lx[:, 7, W - 1] = 0; lx[:, 7, W - 1, 14:] = 63; lm[:, 7, W - 1] = 255
    g[:, 6, :, 15] = 255; lm[:, 6, :, 15] = 255; g[:, 6, :, 14] = 0; lm[:, 6, :, 14] = 0
    return pack(x, g, lx, lm, w, lim)
def setup_inputs_corners(rng):
    pro = rng.integers(0, 64, (8, 1, 16)); lx = near(rng, pro, W, [0, 0, 1]); lx[:, :, 0] = pro[:, 0]
    x = near(rng, pro, K, [0, 1, ND, ND + 1, ND + 2, 16])
    w = rng.integers(0, 256, (8, 16, 2)); w[0] = 0; w[1] = 255; w[2, :, 0] = 0; w[2, :, 1] = 255; w[3, :, 1] = w[3, :, 0]; w[4, :15] = 0; w[4, 15] = 255; w[5, 1:] = 0; w[5, 0] = 255
    w[6] = 255 * rng.integers(0, 2, (16, 2)); w = w[rng.permutation(8)]
    def mean(n):
        return np.where(rng.random((N, 8, n, 1)) < 0.6, 255 * rng.integers(0, 2, (N, 8, n, 1)), rng.integers(0, 256, (N, 8, n, 16)))
    case = (np.arange(8)[None, :] + np.arange(N)[:, None] + rng.integers(0, 5)) % 5; case = case[:, :, None]
    lim = np.where(case == 0, 0, np.where(case == 1, 4081, np.where(case == 2, 4081 * rng.integers(0, 2, (N, 8, 16)), np.where(case == 3, 1, rng.integers(900, 1900, (N, 8, 16))))))
    return pack(x, mean(K), lx, mean(W), w, lim)
def setup_inputs_ties(rng):
    pro = rng.integers(0, 64, (8, 1, 16)); far = np.where(rng.permutation(8) < 4, 0, rng.integers(130, 251, 8)).reshape(8, 1, 1)
    b = rng.integers(0, 255 - far, (8, 1, 16)); side = rng.integers(0, 2, (8, 1, 16))
    x = near(rng, pro, K, [0, 1, 1, 1]); lx = near(rng, pro, W, [0, ND, ND, ND + 1])
    g = b + far * side + rng.integers(0, 2, (N, 8, K, 16)); lm = b + far * (1 - side) + rng.integers(0, 2, (N, 8, W, 16))
    lim = np.where(far[:, 0] == 0, rng.integers(5, 13, (N, 8, 16)), 16 * far[:, 0] + rng.integers(-3, 5, (N, 8, 16)))
    return pack(x, g, lx, lm, rng.integers(0, 256, (8, 16, 2)), lim)
def setup_inputs_alike(rng):
    o = rng.permutation(64); al = o[:4]; kinds = (rng.integers(0, 4, (8, 1, 16)) + (rng.random((8, 6, 16)) < 0.12) * rng.integers(1, 4, (8, 6, 16))) & 3
    pro = al[kinds]; x = near(rng, pro, K, [0]); lx = near(rng, pro, W, [0])
    g = rng.integers(0, 256, (N, 8, K, 16)); lm = rng.integers(0, 256, (N, 8, W, 16)); w = rng.integers(0, 256, (8, 16, 2))
    even = (np.arange(N) % 2 == 0)[:, None, None]
    lim = np.where((rng.random((N, 8, 1)) < 0.6) | even, 4081, rng.integers(900, 1900, (N, 8, 16)))
    two = np.sort(o[4:12].reshape(4, 2), axis=1); spot = np.arange(W); four = [int(e) for e in rng.permutation(8)[:4]]
    for e in four:
        lx[:, e] = pro[e, 0]; lx[:, e, :, 0] = two[spot & 3, 1]; lx[:, e, :, 14] = spot & 63; lx[:, e, :, 15] = spot >> 6
        w[e] = 0; w[e, 14, 0] = 1; w[e, 15, 0] = 64; lim[:, e] = 4081
    for r in range(N):
        j = rng.permutation(W >> 1)[:K]
        put = [4 * (j >> 1) + 2 + (j & 1),
               np.full(K, 4 * rng.integers(0, W >> 2) + 2 + rng.integers(0, 2)),
               4 * rng.permutation(W >> 2)[:K] + (np.arange(K) >= 256),
               np.repeat(4 * rng.permutation(W >> 2)[:K >> 1] + (np.arange(K >> 1) & 3), 2)]
        for e, p in zip(four, put):
            x[r, e] = pro[e, 0]; x[r, e, :, 0] = two[p & 3, 0]; x[r, e, :, 14] = p & 63; x[r, e, :, 15] = p >> 6
    e = four[2]
    g[:, e] = rng.integers(0, 41, (N, K, 16)) + 200 * even; lm[:, e] = rng.integers(0, 41, (N, W, 16)); lim[:, e] = rng.integers(700, 2500, (N, 16))
    return pack(x, g, lx, lm, w, lim)
def check_inputs(d):
    bad = []
    for k, lo, hi in (("xw", 0, 63), ("gw", 0, 255), ("lex", 0, 63), ("mng", 0, 255), ("wts", 0, 255), ("th", 0, 4081)):
        a = np.asarray(d[k]).astype(np.float64)
        if not (np.min(a) >= lo and np.max(a) <= hi): bad.append("range of " + k)
        elif np.any(a != np.floor(a)): bad.append("whole numbers of " + k)
    a = np.asarray(d["wts"])
    if np.any(a != a[:1]): bad.append("wts alike on all ranks")
    return bad
def visit(t, x, g, lx, lm, w, lim):
    p = w[..., :1] * x; u = (np.add.reduce(p, axis=1, keepdims=True) - p) & (W - 1)
    p = w[..., 1:] * x; u2 = (np.add.reduce(p, axis=1, keepdims=True) - p) & (W - 1)
    h = (((u * u2) >> 5) + u) & (W - 1)
    c = np.take_along_axis(lx, h.reshape(8, 1, 16 * K), 2).reshape(8, 16, 16, K)
    m = np.take_along_axis(lm, h.reshape(8, 1, 16 * K), 2).reshape(8, 16, 16, K)
    differ = np.add.reduce((c != x[:, :, None, :]).astype(np.int32), axis=1)
    far = np.add.reduce(np.abs(m - g[:, :, None, :]), axis=1)
    lane = np.arange(16); b = c[:, lane, lane, :]
    pair = (b != x) & (differ <= ND + 1)
    has = np.any(pair, axis=1); f = np.argmax(pair, axis=1)[:, None, :]
    def at(a):
        return np.take_along_axis(a, f, 1)[:, 0]
    xa, xb, hf = at(x), at(b), at(h)
    free = at((far < lim).astype(np.int32)) == 1
    pc = 64 * np.minimum(xa, xb) + np.maximum(xa, xb)
    flag = np.zeros(4096, bool); flag[pc[has & ~free]] = True
    merge = has & free & ~flag[pc]
    mf = np.take_along_axis(lm, hf[:, None, :], 2)
    row = lane[None, :, None]
    xn = np.where((row == f) & merge[:, None, :], np.minimum(x, b), x)
    xn = np.where((row == t) & ~has[:, None, :], b, xn)
    gn = np.where(merge[:, None, :], (g + mf) >> 1, g)
    for e in range(8):
        for i in np.flatnonzero(merge[e])[::-1]:
            lx[e, :, hf[e, i]] = xn[e, :, i]; lm[e, :, hf[e, i]] = gn[e, :, i]
    x[...] = xn; g[...] = gn
def reference(xw, gw, lex, mng, wts, th):
    x = xw.astype(np.float32).astype(np.int32).reshape(N, 8, 16, K); g = gw.astype(np.float32).astype(np.int32).reshape(N, 8, 16, K)
    lx = lex.astype(np.float32).astype(np.int32).reshape(N, 8, 16, W); lm = mng.astype(np.float32).astype(np.int32).reshape(N, 8, 16, W)
    w = wts.astype(np.int32).reshape(N, 8, 16, 2); lim = th.astype(np.int32).reshape(N, 8, 16, 1)
    for t in range(T):
        for r in range(N):
            v = (r + S * t) % N; visit(t, x[r], g[r], lx[v], lm[v], w[v], lim[v])
    return {"yx": x.reshape(N, 128, K).astype(np.float32).astype(BF), "yg": g.reshape(N, 128, K).astype(np.float32).astype(BF),
            "yl": lx.reshape(N, 128, W).astype(np.float32).astype(BF), "ym": np.add.reduce(lm, axis=3).reshape(N, 128, 1).astype(np.float32)}

@@ -1,0 +1,534 @@
+from concourse.mybir import dt, AluOpType, AxisListType, ActivationFunctionType
+
+N, W, K, VIS = 6, 4096, 384, 3
+HBL = [(0, 192), (192, 384)]
+BLK = [(0, 128), (192, 320), (320, 384), (128, 192)]
+NENG = 8
+BF, F32, I32, U16, F16 = "bfloat16", "float32", "int32", "uint16", "float16"
+SCRATCH = {
+    "lx": ("sbuf", [128, W + K], BF), "mn": ("sbuf", [128, W + K], BF),
+    "wti": ("sbuf", [128, 2], I32), "thi": ("sbuf", [128, 1], I32), "pi": ("sbuf", [128, 1], I32), "pj": ("sbuf", [128, 4], I32),
+    "col": ("sbuf", [128, 24], F32), "i64": ("sbuf", [128, 64], BF), "zz": ("sbuf", [128, 48], BF), "one": ("sbuf", [128, 256], BF), "neg": ("sbuf", [128, 64], BF), "C": ("sbuf", [128, 1024], BF), "CA": ("sbuf", [128, 1024], BF), "la": ("sbuf", [128, K], BF),
+    "X16": ("sbuf", [128, 16 * K], BF), "D": ("sbuf", [128, 16 * K], BF), "E": ("sbuf", [128, 24 * K], BF), "UP": ("sbuf", [128, 256], F32), "Mh": ("sbuf", [128, 512], BF),
+    "hi": ("sbuf", [128, K], I32), "hu": ("sbuf", [128, K], U16), "hd": ("sbuf", [128, K], I32), "Lh": ("sbuf", [128, K], F16), "Hb": ("sbuf", [128, K], F16),
+    "le": ("sbuf", [128, 24], U16), "lf": ("sbuf", [128, 24], U16), "lo": ("sbuf", [128, 24], U16),
+    "ab": ("sbuf", [128, 1536], BF), "U": ("sbuf", [128, 1536], BF), "TS": ("sbuf", [128, 64], BF), "TW": ("sbuf", [128, 256], BF),
+    "ya": ("sbuf", [128, 1], F32), "yb": ("sbuf", [128, 1], F32),
+}
+for _n in ("x0 x1 x2 x3 m0 m1 m2 m3 xn0 xn1 xn2 gn0 gn1 gn2 pm Le Fm nb NP Lx d ad LC LCm XB XC lh RF tx M XT gd LB").split():
+    SCRATCH[_n] = ("sbuf", [128, K], BF)
+for _n in ("cg cl cq B Id BmI up L Lm Gm Wv0 Wv1 Wv2 Wa Wb C6 NI4 MI NI16 I14 FLM B64 FAm FBm").split():
+    SCRATCH[_n] = ("sbuf", [128, 128], BF)
+for _n in ("B8 PH MH WFA WFB").split():
+    SCRATCH[_n] = ("sbuf", [128, 8], BF)
+for _n in ("wr3 WR WI WG CK CN").split():
+    SCRATCH[_n] = ("sbuf", [128, 2048], BF)
+for _n in ("sbi SEL").split():
+    SCRATCH[_n] = ("sbuf", [128, 512], BF)
+for _n in ("pr ps pt").split():
+    SCRATCH[_n] = ("sbuf", [128, 256], I32)
+for _n in ("eq cw ge").split():
+    SCRATCH[_n] = ("sbuf", [128, 16], F32)
+for _n in ("ci cim mc rc nf hw hp z z1 z2 z3").split():
+    SCRATCH[_n] = ("sbuf", [128, 24], F32)
+for _b in range(8):
+    SCRATCH["b%d" % _b] = ("psum", [128, 512], F32)
+SEMAPHORES = ["qv", "qs", "qt", "qg", "lx", "lw", "lt", "lg", "ll", "lm", "ax1", "ag1", "ax2", "ag2", "ax3", "ag3", "rl", "ox", "og", "ol", "om"]
+
+
+def rank_program(g, core, T, topo):
+    rank = T.rank_of(core)
+    if rank is None:
+        return
+    A, AF = AluOpType, ActivationFunctionType
+    Q = {"v": g.vector, "s": g.scalar, "t": g.tensor, "g": g, "y": g.sync}
+    own = {"v": "qv", "s": "qs", "t": "qt", "g": "qg"}
+    cnt = {"v": 0, "s": 0, "t": 0, "g": 0}
+    known = {q: {} for q in Q}
+    past = {}
+    acc = {}
+
+    def ref(name, lo=0, hi=None, step=1, p=128):
+        hi = T[name].shape[1] if hi is None else hi
+        return (name, lo, hi, T[name][0:p, lo:hi:step] if step != 1 else T[name][0:p, lo:hi], step)
+
+    def meet(lo, hi, st, l2, h2, s2):
+        return lo < h2 and l2 < hi and not (st == s2 and st > 1 and (lo - l2) % st)
+
+    def is_ps(name):
+        return name in SCRATCH and SCRATCH[name][0] == "psum"
+
+    def need(q, reads, writes):
+        me = own.get(q)
+        dep = {}
+        for rs, w in ((reads, False), (writes, True)):
+            for (name, lo, hi, _, st) in rs:
+                for (l2, h2, ev, c, w2, s2) in acc.get(name, []):
+                    if is_ps(name):
+                        hit = ev != me or (q != "t" and (w or w2) and l2 < hi and lo < h2)
+                    else:
+                        hit = (w or w2) and meet(lo, hi, st, l2, h2, s2)
+                    if hit and dep.get(ev, 0) < c:
+                        dep[ev] = c
+        todo = {e: c for e, c in dep.items() if known[q].get(e, 0) < c}
+        for e in list(todo):
+            if any(f != e and past.get((f, todo[f]), {}).get(e, 0) >= todo[e] for f in todo):
+                del todo[e]
+        for e, c in todo.items():
+            Q[q].wait_ge(T.sem[e], c)
+            k = known[q]
+            k[e] = max(k.get(e, 0), c)
+            for e2, c2 in past.get((e, c), {}).items():
+                k[e2] = max(k.get(e2, 0), c2)
+
+    def note(ev, c, q, reads, writes):
+        k = dict(known[q]) if q else {}
+        k[ev] = c
+        past[(ev, c)] = k
+        for rs, w in ((reads, False), (writes, True)):
+            for (name, lo, hi, _, st) in rs:
+                old = acc.get(name, [])
+
+                def inside(o):
+                    return lo <= o[0] and o[1] <= hi and (st == 1 or (st == o[5] and (lo - o[0]) % st == 0))
+                if w:
+                    old = [o for o in old if not inside(o) or (is_ps(name) and o[2] != ev)]
+                else:
+                    old = [o for o in old if not (o[2] == ev and not o[4] and inside(o))]
+                acc[name] = old + [(lo, hi, ev, c, w, st)]
+
+    def do(q, fn, reads, writes):
+        need(q, reads, writes)
+        ins = fn()
+        cnt[q] += 1
+        ins.then_inc(T.sem[own[q]], 1)
+        note(own[q], cnt[q], q, reads, writes)
+
+    def rd(*xs):
+        out = []
+        for x in xs:
+            if isinstance(x, tuple):
+                out += x[1] if x[0] is None else [x]
+        return out
+
+    def ap(x):
+        return x[3] if isinstance(x, tuple) else x
+
+    def ind(win, off):
+        return (None, [win, off], None, win[3].indirect(off[3]))
+
+    def tt(out, a, b, op):
+        do("v", lambda: g.vector.tensor_tensor(ap(out), ap(a), ap(b), op), rd(a, b), rd(out))
+
+    def ts(out, a, s1, op0, s2=None, op1=None):
+        if op1 is None:
+            do("v", lambda: g.vector.tensor_scalar(ap(out), ap(a), ap(s1), None, op0), rd(a, s1), rd(out))
+        else:
+            do("v", lambda: g.vector.tensor_scalar(ap(out), ap(a), ap(s1), ap(s2), op0, op1), rd(a, s1, s2), rd(out))
+
+    def cp(out, a):
+        do("v", lambda: g.vector.tensor_copy(ap(out), ap(a)), rd(a), rd(out))
+
+    def fill(out, c):
+        do("v", lambda: g.vector.memset(ap(out), c), [], rd(out))
+
+    def act(out, a, f, bias=0.0, scale=1.0, accum=None):
+        if accum is None:
+            do("s", lambda: g.scalar.activation(ap(out), ap(a), f, bias=ap(bias), scale=ap(scale)), rd(a, bias, scale), rd(out))
+        else:
+            do("s", lambda: g.scalar.activation(ap(out), ap(a), f, bias=ap(bias), scale=ap(scale), accum_out=ap(accum)), rd(a, bias, scale), rd(out, accum))
+
+    def mm(out, l, r, start, stop):
+        do("t", lambda: g.tensor.matmul(ap(out), ap(l), ap(r), start, stop), rd(l, r), rd(out))
+
+    def iota(out, pattern, base, cm, small=True):
+        if small:
+            do("g", lambda: g.iota(ap(out), pattern, base, cm, allow_small_or_imprecise_dtypes=True), [], rd(out))
+        else:
+            do("g", lambda: g.iota(ap(out), pattern, base, cm), [], rd(out))
+
+    def load(q, out, src, sem):
+        Q[q].dma_start(ap(out), src).then_inc(T.sem[sem], 16)
+        note(sem, 16, None, [], rd(out))
+
+    def store(q, dst, src, sem):
+        need(q, rd(src), [])
+        Q[q].dma_start(dst, ap(src)).then_inc(T.sem[sem], 16)
+        note(sem, 16, q, rd(src), [])
+
+    sent = [0]
+
+    def send(src, dst, to, sem):
+        c = T.cores[to]
+        m = 0
+        for e in topo.engines(core, c)[:NENG]:
+            m |= 1 << e
+        rid, pid, _ = topo.addr(c)
+        need("g", rd(src), [])
+        g.remote_dma(ap(dst), ap(src), T.sem[sem], T.sem["rl"], pid, rid, m)
+        sent[0] += NENG
+
+    load("y", ref("x0"), T.xw[:, :], "lx")
+    load("y", ref("wti"), T.wts[:, :], "lw")
+    load("s", ref("lx", 0, W), T.lex[:, :], "ll")
+    load("y", ref("m0"), T.gw[:, :], "lg")
+    load("y", ref("thi"), T.th[:, :], "lt")
+    load("s", ref("mn", 0, W), T.mng[:, :], "lm")
+    for t in (1, 2, 3):
+        note("ax%d" % t, NENG, None, [], [ref("x%d" % t)])
+        note("ag%d" % t, NENG, None, [], [ref("m%d" % t)])
+
+    iota(ref("pi"), [[1, 1]], 0, 1, False)
+    iota(ref("cq"), [[1, 128]], 0, 0)
+    iota(ref("cg"), [[1, 8], [0, 16]], 0, 0)
+    iota(ref("cl"), [[0, 8], [1, 16]], 0, 0)
+    iota(ref("i64"), [[1, 64]], 0, 0)
+    iota(ref("ci"), [[16, 24]], 4096, 0)
+    iota(ref("wr3"), [[-100, 16], [1, 8], [100, 16]], 0, 0)
+    iota(ref("sbi"), [[16, 4], [0, 8], [1, 16]], 0, 0)
+
+    def col(j):
+        return ref("col", j, j + 1)
+    PG, PL, PP, PLM, THR, W1, W2, THA, THB, C_FAM, C_FBM, C_WA = 0, 1, 2, 3, 4, 7, 8, 9, 10, 11, 12, 13
+    B, Id = ref("B"), ref("Id")
+    ts(ref("pj", 0, 1), ref("pi"), 4, A.arith_shift_right)
+    ts(ref("pj", 1, 2), ref("pi"), 15, A.bitwise_and)
+    fill(ref("C6"), 6144.0)
+    fill(ref("one"), 1.0)
+    fill(ref("zz"), 0.0)
+    fill(ref("neg"), -1.0 / 128)
+    cp(col(PG), ref("pj", 0, 1))
+    cp(col(PL), ref("pj", 1, 2))
+    cp(col(PP), ref("pi"))
+    ts(Id, ref("cq"), col(PP), A.is_equal)
+    ts(B, ref("cg"), col(PG), A.is_equal)
+    act(ref("NI4"), Id, AF.Copy, scale=-4096.0)
+    tt(ref("BmI"), B, Id, A.subtract)
+    ts(ref("eq"), ref("cl", 0, 16), col(PL), A.is_equal)
+    fill(ref("CK"), 0.0)
+    ts(ref("cw"), ref("eq"), -17.0, A.mult, 1.0, A.add)
+    cp(ref("B8"), ref("B", 0, 128, 16))
+    cp(ref("col", W1, W1 + 2), ref("wti"))
+    ts(ref("Wa"), ref("BmI"), col(W1), A.mult)
+    ts(ref("Wb"), ref("BmI"), col(W2), A.mult)
+    for k in range(16):
+        ts(ref("CK", 129 * k, 128 * k + 128, 16), ref("B8"), ref("cw", k, k + 1), A.mult)
+
+    def more_constants():
+        for name, src, s in (("MI", "Id", -1.0), ("NI16", "Id", -16.0),
+                             ("I14", "Id", 2.0 ** -14), ("FLM", "B", 2.0 ** 18), ("B64", "B", 64.0), ("PH", "B8", 0.5), ("MH", "B8", -0.5)):
+            act(ref(name), ref(src), AF.Copy, scale=s)
+        act(ref("CN"), ref("CK"), AF.Copy, scale=-1.0)
+
+    def picks(mat, scale):
+        act(ref(mat), ref("wr3"), AF.Copy, scale=0.0)
+        for r in range(16):
+            act(ref(mat, 129 * r, 128 * r + 128, 16), ref("B8"), AF.Copy, scale=ref(scale, r, r + 1))
+
+    def v_constants():
+        ts(ref("up"), ref("cl"), col(PL), A.is_gt)
+        ts(ref("pj", 2, 3), ref("thi"), 4, A.arith_shift_right)
+        ts(ref("pj", 3, 4), ref("thi"), 15, A.bitwise_and)
+        ts(col(THR), col(PL), 0.0, A.not_equal)
+        tt(ref("L"), ref("up"), B, A.mult)
+        ts(ref("WR"), ref("wr3"), col(PG), A.is_equal)
+        cp(ref("col", THA, THA + 2), ref("pj", 2, 4))
+        ts(ref("Lm"), ref("L"), -128.0, A.mult)
+        tt(ref("Gm"), ref("BmI"), ref("L"), A.subtract)
+        ts(col(PLM), col(PL), -1.0, A.mult, 3072.0, A.add)
+        ts(col(C_FAM), col(THA), -16.0, A.mult)
+        ts(col(C_FBM), col(THB), -1.0, A.mult)
+        tt(ref("Wv0"), ref("Lm"), Id, A.add)
+        ts(ref("Gm"), ref("Gm"), 2.0 ** -14, A.mult)
+        ts(col(C_WA), col(THA), -16.0, A.mult, 4096.0, A.add)
+        ts(ref("FAm"), B, col(C_FAM), A.mult, 64.0, A.mult)
+        ts(ref("FBm"), B, col(C_FBM), A.mult, 64.0, A.mult)
+        tt(ref("Wv0", 0, 128, 16), ref("Wv0", 0, 128, 16), ref("Gm", 0, 128, 16), A.subtract)
+        ts(ref("WFA"), ref("B8"), col(C_WA), A.mult)
+        ts(ref("WFB"), ref("B8"), col(C_FBM), A.mult)
+
+    def late_constants():
+        for t in range(1, VIS):
+            tt(ref("Wv%d" % t), ref("Lm"), Id, A.add)
+            ts(col(THR + t), col(PL), float(t), A.not_equal)
+        ts(ref("SEL", p=64), ref("sbi", p=64), ref("col", PP, PP + 1, p=64), A.is_equal)
+        for t in range(1, VIS):
+            w = ref("Wv%d" % t, t, 128, 16)
+            tt(w, w, ref("Gm", t, 128, 16), A.subtract)
+        ts(ref("cim"), ref("ci"), col(PL), A.add)
+        ts(ref("ge"), ref("cl", 0, 16), col(PL), A.is_le, -65536.0, A.mult)
+
+    def full(b, n=K):
+        return ref("b%d" % b, 0, n)
+
+    def wrap(out, mat, src, first, last):
+        for r in range(16):
+            mm(out, ref(mat, 128 * r, 128 * r + 128), ref(src, r, K, 16), first and r == 0, last and r == 15)
+
+    lexw, mngw = ref("lx", 0, W), ref("mn", 0, W)
+
+    def spread(t, b, on_v):
+        i0, i1 = BLK[b]
+        for k in range(16):
+            o, s = ref("X16", 16 * i0 + k, 16 * i1, 16), ref("x%d" % t, i0, i1)
+            if on_v:
+                cp(o, s)
+            else:
+                act(o, s, AF.Copy)
+
+    def hash_s(t, b):
+        hash_1(t, b)
+        hash_2(b)
+        hash_3(b)
+
+    def hash_1(t, b):
+        i0, i1 = HBL[b]
+        n = i1 - i0
+        xs = ref("x%d" % t, i0, i1)
+        mm(ref("b0", 0, n), ref("Wa"), xs, True, True)
+        mm(ref("b0", n, 2 * n), ref("Wb"), xs, True, True)
+        mm(full(2, n), ref("Wb"), xs, True, False)
+        mm(full(1, n), ref("C6"), ref("one", 0, n), True, False)
+        mm(full(1, n), ref("Wa"), xs, False, False)
+
+    def hash_2(b):
+        n = HBL[b][1] - HBL[b][0]
+        act(ref("Mh", 0, 2 * n), ref("b0", 0, 2 * n), AF.Identity, bias=192.0 - 4095.0 / 8192.0, scale=1.0 / 4096.0)
+
+    def hash_3(b):
+        n = HBL[b][1] - HBL[b][0]
+        mm(full(2, n), ref("NI4"), ref("Mh", n, 2 * n), False, True)
+        mm(full(1, n), ref("NI4"), ref("Mh", 0, n), False, True)
+        act(ref("UP", 0, n), full(2, n), AF.Identity, bias=786432.0)
+
+    def hash_v(b):
+        i0, i1 = HBL[b]
+        n = i1 - i0
+        hv = [(0, n // 2), (n // 2, n)]
+        for a, e in hv:
+            tt(ref("pr", a, e), ref("UP", a, e), ref("b1", a, e), A.mult)
+        for a, e in hv:
+            ts(ref("ps", a, e), ref("pr", a, e), 5, A.arith_shift_right)
+        for a, e in hv:
+            tt(ref("pt", a, e), ref("ps", a, e), ref("b1", a, e), A.add)
+        for a, e in hv:
+            ts(ref("hi", i0 + a, i0 + e), ref("pt", a, e), 4095, A.bitwise_and)
+        for a, e in hv:
+            cp(ref("hu", i0 + a, i0 + e), ref("hi", i0 + a, i0 + e))
+
+    def pick(i0, i1):
+        tt(ref("D", 16 * i0, 16 * i1), ind(lexw, ref("hu", i0, i1)), ref("X16", 16 * i0, 16 * i1), A.not_equal)
+
+    def count(b):
+        i0, i1 = BLK[b]
+        for k in range(16):
+            mm(ref("b3", i0, i1), ref("CK", 128 * k, 128 * k + 128), ref("D", 16 * i0 + k, 16 * i1, 16), k == 0, k == 15)
+
+    def look_s(t, b):
+        i0, i1 = BLK[b]
+        n = i1 - i0
+        w, o = lexw, ref("hu", i0, i1)
+        do("s", lambda: g.scalar.activation(ref("C")[3], w[3].indirect(o[3]), AF.Copy), [w, o], [ref("C")])
+        for h in range(2):
+            for k in range(8):
+                c = ref("b%d" % (6 + h), n * k, n * k + n)
+                mm(c, ref("MI"), ref("x%d" % t, i0, i1), True, False)
+                mm(c, Id, ref("C", 8 * h + k, 1024, 16), False, True)
+
+    def unlike_s():
+        for h in range(2):
+            act(ref("CA", 512 * h, 512 * h + 512), full(6 + h, 512), AF.Abs)
+        act(ref("C"), ref("CA"), AF.Relu, bias=1.0, scale=-1.0)
+
+    def count_s(b):
+        i0, i1 = BLK[b]
+        n = i1 - i0
+        mm(ref("b3", i0, i1), ref("one", 0, 128), ref("neg", 0, n), True, False)
+        for h in range(2):
+            for k in range(8):
+                j = 8 * h + k
+                mm(ref("b3", i0, i1), ref("CN", 128 * j, 128 * j + 128), ref("C", n * j, n * j + n), False, j == 15)
+
+    def scatter(buf, src):
+        w, o, s = ref(buf), ref("lo"), ref(src)
+        do("v", lambda: g.vector.tensor_copy(w[3].indirect(o[3]), s[3]), [o, s], [w])
+
+    hash_s(0, 0)
+    spread(0, 0, True)
+    hash_v(0)
+    for t in range(VIS):
+        x, m, last = "x%d" % t, "m%d" % t, t == VIS - 1
+        xn, gn = "xn%d" % t, "gn%d" % t
+        to = (rank + 2) % N if last else (rank - 1) % N
+
+        hash_s(t, 1)
+        i0, i1 = HBL[1]
+        n = i1 - i0
+        pick(0, 32)
+        tt(ref("pr", 0, n), ref("UP", 0, n), full(1, n), A.mult)
+        pick(32, 64)
+        ts(ref("ps", 0, n), ref("pr", 0, n), 5, A.arith_shift_right)
+        pick(64, 96)
+        tt(ref("pt", 0, n), ref("ps", 0, n), full(1, n), A.add)
+        pick(96, 128)
+        ts(ref("hi", i0, i1), ref("pt", 0, n), 4095, A.bitwise_and)
+        ts(full(5, i0), ref("hi", 0, i0), -2048.0, A.add)
+        cp(ref("hu", i0, i1), ref("hi", i0, i1))
+        count(0)
+        spread(t, 1, False)
+        if t == 0:
+            more_constants()
+        look_s(t, 3)
+        spread(t, 2, False)
+        unlike_s()
+        act(full(4), ref(x), AF.Copy)
+        pick(*BLK[1])
+        count(1)
+        count_s(3)
+        pick(*BLK[2])
+        count(2)
+        if t == 0:
+            v_constants()
+            picks("WI", "eq")
+        ts(ref("b5", i0, i1), ref("hi", i0, i1), -2048.0, A.add)
+        if t > 0:
+            scatter("mn", "gn%d" % (t - 1))
+
+        ts(ref("pm"), full(3), -13.5, A.is_le)
+        mm(full(0), ref("Wv%d" % t), ref("pm"), True, True)
+        halves = [(0, K // 2), (K // 2, K)]
+        for a, e in halves:
+            ts(ref("Le", a, e), ref("b0", a, e), col(THR + t), A.is_ge)
+        act(ref("nb"), full(0), AF.Abs, bias=col(THR + t))
+        act(ref("Fm"), full(0), AF.Relu)
+        for a, e in halves:
+            tt(ref("Lh", a, e), ref("Le", a, e), ref("b5", a, e), A.mult)
+        tt(ref("Lx"), ref("Le"), full(4), A.mult)
+        wl = ref("b2", 0, 24)
+        wrap(wl, "WR", "Lh", True, True)
+        mm(full(1), B, ref("Lx"), True, True)
+        act(ref("NP"), ref("nb"), AF.Relu, bias=64.0, scale=-2.0 ** 20)
+        ts(ref("le"), wl, 2048.0, A.add)
+        ts(ref("hw"), wl, -16384.0, A.add)
+        act(ref("XB"), full(1), AF.Identity, bias=192.0 - 15.0 / 32.0, scale=1.0 / 16.0)
+        wm = ref("b2", 0, 24)
+        mm(wm, B, ref("zz", 0, 24), True, False)
+        for c in range(3):
+            o, fc = ref("b2", 8 * c, 8 * c + 8), ref("Fm", 128 * c, 128 * c + 128)
+            mm(o, fc, ref("WFA"), False, False)
+            mm(o, fc, ref("WFB"), False, False)
+        mm(ref("b3", 0, 48), B, ref("zz"), True, False)
+        for c in range(3):
+            lxc = ref("Lx", 128 * c, 128 * c + 128)
+            mm(ref("b3", 8 * c, 8 * c + 8), lxc, ref("MH"), False, False)
+            mm(ref("b3", 24 + 8 * c, 32 + 8 * c), lxc, ref("PH"), False, False)
+        mm(full(6), Id, ref("Lx"), True, False)
+        mm(full(6), Id, ref("NP"), False, True)
+        mm(full(0), Id, ref(x), True, False)
+        mm(full(0), ref("MI"), ref("NP"), False, True)
+
+        tt(ref("d"), ind(mngw, ref("le")), ref(m), A.subtract)
+        act(ref("ad"), ref("d"), AF.Abs)
+        tt(ref("LC"), ind(lexw, ref("le")), ref("Le"), A.mult)
+        act(ref("XC"), ref("XB"), AF.Copy, scale=64.0)
+        if t == 0:
+            late_constants()
+        wl2 = ref("b7", 0, 24)
+        for c in range(3):
+            mm(ref("b2", 8 * c, 8 * c + 8), ref("ad", 128 * c, 128 * c + 128), ref("B8"), False, c == 2)
+        for c in range(3):
+            lcc = ref("LC", 128 * c, 128 * c + 128)
+            mm(ref("b3", 8 * c, 8 * c + 8), lcc, ref("MH"), False, False)
+            mm(ref("b3", 24 + 8 * c, 32 + 8 * c), lcc, ref("MH"), False, c == 2)
+        act(ref("mc"), ref("b3", 0, 24), AF.Copy)
+        act(ref("rc"), ref("b3", 24, 48), AF.Abs)
+        ts(ref("hd"), ref("d"), 0.5, A.mult, -0.25, A.add)
+        tt(ref("LCm"), ref("LC"), full(6), A.min)
+        ts(ref("nf"), ref("b2", 0, 24), 4095.5, A.is_ge)
+        wrap(wl2, "WI", "XC", True, False)
+        for q in range(24):
+            act(ref("ab", 64 * q, 64 * q + 64), ref("i64"), AF.Abs, bias=ref("mc", q, q + 1))
+
+        for q in range(24):
+            u = ref("U", 64 * q, 64 * q + 64)
+            ts(u, ref("ab", 64 * q, 64 * q + 64), ref("rc", q, q + 1), A.is_equal, ref("nf", q, q + 1), A.mult)
+            mm(ref("b1", 0, 64, p=64), u, u, q == 0, q == 23)
+            if q == 7:
+                mm(full(6), B, ref("Lx"), True, False)
+                mm(full(6), ref("NI16"), ref("XB"), False, True)
+        act(ref("XT"), full(0), AF.Copy)
+        act(ref("la"), full(6), AF.Abs, bias=col(PLM))
+        wrap(wl2, "WR", "LC", False, True)
+        ts(ref("TS", p=64), ref("b1", 0, 64, p=64), 1.0, A.min)
+        ts(ref("lf"), wl2, -12288.0, A.add)
+        for b in range(4):
+            mm(ref("b2", 64 * b, 64 * b + 64), ref("SEL", 128 * b, 128 * b + 128, p=64), ref("TS", p=64), True, True)
+        act(ref("lh"), ref("la"), AF.Relu, bias=1.0, scale=-1.0)
+        if t == 0:
+            picks("WG", "ge")
+        mm(full(3), B, ref("Lh"), True, True)
+        for lw, src in (("B64", "Le"), ("FAm", "Fm"), ("FBm", "Fm"), ("B64", "ad")):
+            mm(full(5), ref(lw), ref(src), src == "Le", False)
+        cp(ref("TW"), ref("b2", 0, 256))
+        tt(ref("RF"), ind(ref("TW"), ref("lf")), ref("lh"), A.mult)
+        cp(ref("Hb"), full(3))
+        mm(full(5), ref("FLM"), ref("RF"), False, True)
+        mm(full(4), Id, ref(x), True, False)
+        mm(full(4), ref("MI"), ref("Lx"), False, False)
+        mm(full(4), Id, ref("LCm"), False, True)
+        wl3 = ref("b2", 0, 24)
+        mm(full(6), Id, ref(m), True, False)
+
+        ts(ref("M"), full(5), 32.0, A.is_lt, 16384.0, A.mult)
+        wrap(wl3, "WI", "M", True, True)
+        act(full(1), ref("M"), AF.Copy)
+        for a, e in halves:
+            tt(ref("tx", a, e), ref("XT", a, e), ref("b5", a, e), A.min)
+        for a, e in halves:
+            tt(ref(xn, a, e), ref("tx", a, e), ref("b4", a, e), A.max)
+        send(ref(xn), ref("x%d" % (t + 1)), to, "ax%d" % (t + 1))
+        tt(ref("hp"), ref("hw"), wl3, A.add)
+        ts(ref("z3"), wl3, -2.0, A.mult, 34816.0, A.add)
+        for q in range(24):
+            n, e = K - 16 * q, 384 * q
+            ts(ref("E", e, e + n), ref("Hb", 16 * q, K), ref("hp", q, q + 1), A.is_equal)
+            mm(ref("b7", 16 * q, K), B, ref("E", e, e + n), q == 0, q == 23)
+            if q == 5:
+                tt(ref("z3"), ref("z3"), ref("hp"), A.add)
+            if q == 8:
+                tt(ref("gd"), ref("hd"), full(1), A.mult)
+            if q == 11:
+                tt(ref("z"), ref("z3"), ref("cim"), A.min)
+        act(ref("LB"), full(7), AF.Copy, scale=65536.0)
+        wl4 = ref("b5", 0, 24)
+        for r in range(16):
+            mm(wl4, ref("WG", 128 * r, 128 * r + 128), ref("E", r, 24 * K, K), r == 0, False)
+        wrap(wl4, "WI", "LB", False, True)
+        mm(full(6), ref("I14"), ref("gd"), False, True)
+        act(ref(gn), full(6), AF.Copy)
+        send(ref(gn), ref("m%d" % (t + 1)), to, "ag%d" % (t + 1))
+        if not last:
+            hash_s(t + 1, 0)
+            spread(t + 1, 0, False)
+        tt(ref("z1"), ref("cim"), wl4, A.min)
+        tt(ref("z2"), ref("z1"), ref("z"), A.max)
+        cp(ref("lo"), ref("z2"))
+        scatter("lx", xn)
+        if last:
+            store("y", T.yl[:, :], lexw, "ol")
+            scatter("mn", gn)
+        else:
+            hash_v(0)
+
+    half = W // 2
+    act(ref("D", 0, half), ref("mn", 0, half), AF.Copy, accum=ref("ya"))
+    do("v", lambda: g.vector.tensor_reduce(ref("yb")[3], ref("mn", half, W)[3], AxisListType.X, A.add), [ref("mn", half, W)], [ref("yb")])
+    tt(ref("ya"), ref("ya"), ref("yb"), A.add)
+    store("y", T.yx[:, :], ref("x3"), "ox")
+    store("y", T.yg[:, :], ref("m3"), "og")
+    store("y", T.ym[:, :], ref("ya"), "om")
+    for q in ("v", "s", "t", "g"):
+        g.wait_ge(T.sem[own[q]], cnt[q])
+    g.wait_ge(T.sem["rl"], sent[0])
+    for s in ("ox", "og", "ol", "om"):
+        g.wait_ge(T.sem[s], 16)

@@ -1,35 +1,36 @@
 from concourse.mybir import dt, AluOpType, AxisListType, ActivationFunctionType
 
 N, W, K, VIS = 6, 4096, 384, 3
-HBL = [(0, 192), (192, 384)]
-BLK = [(0, 128), (192, 320), (320, 384), (128, 192)]
+CH = 128
 NENG = 8
+SUMV = 1408
 BF, F32, I32, U16, F16 = "bfloat16", "float32", "int32", "uint16", "float16"
 SCRATCH = {
-    "lx": ("sbuf", [128, W + K], BF), "mn": ("sbuf", [128, W + K], BF),
+    "lx": ("sbuf", [128, K + W], BF), "mn": ("sbuf", [128, K + W], BF),
     "wti": ("sbuf", [128, 2], I32), "thi": ("sbuf", [128, 1], I32), "pi": ("sbuf", [128, 1], I32), "pj": ("sbuf", [128, 4], I32),
-    "col": ("sbuf", [128, 24], F32), "i64": ("sbuf", [128, 64], BF), "zz": ("sbuf", [128, 48], BF), "one": ("sbuf", [128, 256], BF), "neg": ("sbuf", [128, 64], BF), "C": ("sbuf", [128, 1024], BF), "CA": ("sbuf", [128, 1024], BF), "la": ("sbuf", [128, K], BF),
-    "X16": ("sbuf", [128, 16 * K], BF), "D": ("sbuf", [128, 16 * K], BF), "E": ("sbuf", [128, 24 * K], BF), "UP": ("sbuf", [128, 256], F32), "Mh": ("sbuf", [128, 512], BF),
-    "hi": ("sbuf", [128, K], I32), "hu": ("sbuf", [128, K], U16), "hd": ("sbuf", [128, K], I32), "Lh": ("sbuf", [128, K], F16), "Hb": ("sbuf", [128, K], F16),
+    "col": ("sbuf", [128, 24], F32), "i64": ("sbuf", [128, 64], BF), "one": ("sbuf", [128, 128], BF),
+    "X16": ("sbuf", [128, 16 * CH], BF), "C": ("sbuf", [128, 16 * K], BF), "D": ("sbuf", [128, 16 * K], BF), "E": ("sbuf", [128, 24 * CH], BF),
+    "UP": ("sbuf", [128, K], F32), "Mh": ("sbuf", [128, 2 * K], BF),
+    "hu": ("sbuf", [128, K], U16), "hf": ("sbuf", [128, K], F16), "Lh": ("sbuf", [128, K], F16), "Hb": ("sbuf", [128, K], F16),
     "le": ("sbuf", [128, 24], U16), "lf": ("sbuf", [128, 24], U16), "lo": ("sbuf", [128, 24], U16),
     "ab": ("sbuf", [128, 1536], BF), "U": ("sbuf", [128, 1536], BF), "TS": ("sbuf", [128, 64], BF), "TW": ("sbuf", [128, 256], BF),
-    "ya": ("sbuf", [128, 1], F32), "yb": ("sbuf", [128, 1], F32),
+    "ya": ("sbuf", [128, 1], F32), "yb": ("sbuf", [128, 1], F32), "CK": ("sbuf", [128, 2048], BF), "Z": ("sbuf", [128, 144], BF),
+    "mr": ("sbuf", [128, 48], F32), "XB": ("sbuf", [128, 24], BF), "PP": ("sbuf", [128, 16], BF), "PM": ("sbuf", [128, 16], BF),
+    "sj": ("sbuf", [128, K], F32), "run": ("sbuf", [128, SUMV], F32),
 }
-for _n in ("x0 x1 x2 x3 m0 m1 m2 m3 xn0 xn1 xn2 gn0 gn1 gn2 pm Le Fm nb NP Lx d ad LC LCm XB XC lh RF tx M XT gd LB").split():
+for _n in ("x0 x1 x2 x3 m0 m1 m2 m3 xn0 xn1 xn2 gn0 gn1 gn2 pm Le Fm Fx d ad LC ha Zf Xf xp RF M gd O rs rs0 mk mk0").split():
     SCRATCH[_n] = ("sbuf", [128, K], BF)
-for _n in ("cg cl cq B Id BmI up L Lm Gm Wv0 Wv1 Wv2 Wa Wb C6 NI4 MI NI16 I14 FLM B64 FAm FBm").split():
+for _n in ("cg cl cq B Id BmI L G WF WX Wv0 Wv1 Wv2 Wa Wb C6 NI4 MI NB B8K NB8K I8K BmI8K HI NHI NB128 I64 EQ").split():
     SCRATCH[_n] = ("sbuf", [128, 128], BF)
-for _n in ("B8 PH MH WFA WFB").split():
+for _n in ("B8 WFA WFB").split():
     SCRATCH[_n] = ("sbuf", [128, 8], BF)
-for _n in ("wr3 WR WI WG CK CN").split():
-    SCRATCH[_n] = ("sbuf", [128, 2048], BF)
 for _n in ("sbi SEL").split():
     SCRATCH[_n] = ("sbuf", [128, 512], BF)
-for _n in ("pr ps pt").split():
-    SCRATCH[_n] = ("sbuf", [128, 256], I32)
-for _n in ("eq cw ge").split():
+for _n in ("pr ps pt hi").split():
+    SCRATCH[_n] = ("sbuf", [128, K], I32)
+for _n in ("eq cw").split():
     SCRATCH[_n] = ("sbuf", [128, 16], F32)
-for _n in ("ci cim mc rc nf hw hp z z1 z2 z3").split():
+for _n in ("ci cim nf z").split():
     SCRATCH[_n] = ("sbuf", [128, 24], F32)
 for _b in range(8):
     SCRATCH["b%d" % _b] = ("psum", [128, 512], F32)
@@ -132,6 +133,9 @@ def rank_program(g, core, T, topo):
     def fill(out, c):
         do("v", lambda: g.vector.memset(ap(out), c), [], rd(out))
 
+    def scan(out, a, b, op0, op1):
+        do("v", lambda: g.vector.tensor_tensor_scan(ap(out), ap(a), ap(b), 0.0, op0, op1), rd(a, b), rd(out))
+
     def act(out, a, f, bias=0.0, scale=1.0, accum=None):
         if accum is None:
             do("s", lambda: g.scalar.activation(ap(out), ap(a), f, bias=ap(bias), scale=ap(scale)), rd(a, bias, scale), rd(out))
@@ -141,11 +145,18 @@ def rank_program(g, core, T, topo):
     def mm(out, l, r, start, stop):
         do("t", lambda: g.tensor.matmul(ap(out), ap(l), ap(r), start, stop), rd(l, r), rd(out))
 
+    def group(out, terms, first=True, last=True):
+        for j, (l, r) in enumerate(terms):
+            mm(out, ref(l) if isinstance(l, str) else l, r, first and j == 0, last and j == len(terms) - 1)
+
     def iota(out, pattern, base, cm, small=True):
         if small:
             do("g", lambda: g.iota(ap(out), pattern, base, cm, allow_small_or_imprecise_dtypes=True), [], rd(out))
         else:
             do("g", lambda: g.iota(ap(out), pattern, base, cm), [], rd(out))
+
+    def keep_where(out, a, pattern, op, other, cm):
+        do("g", lambda: g.affine_select(ap(out), ap(a), pattern, op, other, 0, cm), rd(a), rd(out))
 
     def load(q, out, src, sem):
         Q[q].dma_start(ap(out), src).then_inc(T.sem[sem], 16)
@@ -168,365 +179,424 @@ def rank_program(g, core, T, topo):
         g.remote_dma(ap(dst), ap(src), T.sem[sem], T.sem["rl"], pid, rid, m)
         sent[0] += NENG
 
+    lexw, mngw = ref("lx", K, K + W), ref("mn", K, K + W)
+
     load("y", ref("x0"), T.xw[:, :], "lx")
     load("y", ref("wti"), T.wts[:, :], "lw")
-    load("s", ref("lx", 0, W), T.lex[:, :], "ll")
+    load("s", lexw, T.lex[:, :], "ll")
     load("y", ref("m0"), T.gw[:, :], "lg")
     load("y", ref("thi"), T.th[:, :], "lt")
-    load("s", ref("mn", 0, W), T.mng[:, :], "lm")
+    load("s", mngw, T.mng[:, :], "lm")
     for t in (1, 2, 3):
         note("ax%d" % t, NENG, None, [], [ref("x%d" % t)])
         note("ag%d" % t, NENG, None, [], [ref("m%d" % t)])
 
+    def col(j):
+        return ref("col", j, j + 1)
+    PG, PL, PP, CF, THR, W1, W2, THA, THB, TH, BF8, BFX, BZ, C_WA, C_WB, THB0 = 0, 1, 2, 3, 4, 7, 8, 9, 10, 11, 12, 13, 14, 15, 16, 17
+    B, Id = ref("B"), ref("Id")
+    BIG = 8192.0
     iota(ref("pi"), [[1, 1]], 0, 1, False)
     iota(ref("cq"), [[1, 128]], 0, 0)
     iota(ref("cg"), [[1, 8], [0, 16]], 0, 0)
-    iota(ref("cl"), [[0, 8], [1, 16]], 0, 0)
-    iota(ref("i64"), [[1, 64]], 0, 0)
-    iota(ref("ci"), [[16, 24]], 4096, 0)
-    iota(ref("wr3"), [[-100, 16], [1, 8], [100, 16]], 0, 0)
-    iota(ref("sbi"), [[16, 4], [0, 8], [1, 16]], 0, 0)
-
-    def col(j):
-        return ref("col", j, j + 1)
-    PG, PL, PP, PLM, THR, W1, W2, THA, THB, C_FAM, C_FBM, C_WA = 0, 1, 2, 3, 4, 7, 8, 9, 10, 11, 12, 13
-    B, Id = ref("B"), ref("Id")
+    iota(ref("cl", 0, 16), [[1, 16]], 0, 0)
+    fill(ref("CK"), 0.0)
     ts(ref("pj", 0, 1), ref("pi"), 4, A.arith_shift_right)
     ts(ref("pj", 1, 2), ref("pi"), 15, A.bitwise_and)
     fill(ref("C6"), 6144.0)
     fill(ref("one"), 1.0)
-    fill(ref("zz"), 0.0)
-    fill(ref("neg"), -1.0 / 128)
-    cp(col(PG), ref("pj", 0, 1))
-    cp(col(PL), ref("pj", 1, 2))
     cp(col(PP), ref("pi"))
+    cp(ref("col", PG, PG + 2), ref("pj", 0, 2))
+    fill(ref("Z"), 0.0)
     ts(Id, ref("cq"), col(PP), A.is_equal)
     ts(B, ref("cg"), col(PG), A.is_equal)
+    ts(ref("eq"), ref("cl", 0, 16), col(PL), A.is_equal)
+    fill(ref("O", 0, 16), 0.0)
+    ts(col(CF), col(PL), -64.0, A.mult, 0.5, A.add)
     act(ref("NI4"), Id, AF.Copy, scale=-4096.0)
     tt(ref("BmI"), B, Id, A.subtract)
-    ts(ref("eq"), ref("cl", 0, 16), col(PL), A.is_equal)
-    fill(ref("CK"), 0.0)
     ts(ref("cw"), ref("eq"), -17.0, A.mult, 1.0, A.add)
     cp(ref("B8"), ref("B", 0, 128, 16))
     cp(ref("col", W1, W1 + 2), ref("wti"))
+    ts(col(THB0), col(CF), -1.0, A.mult, 0.5, A.add)
+    ts(col(BF8), col(CF), BIG, A.mult)
+    ts(col(BFX), col(CF), 128.0, A.mult, -64.0, A.add)
     ts(ref("Wa"), ref("BmI"), col(W1), A.mult)
     ts(ref("Wb"), ref("BmI"), col(W2), A.mult)
-    for k in range(16):
-        ts(ref("CK", 129 * k, 128 * k + 128, 16), ref("B8"), ref("cw", k, k + 1), A.mult)
+    for name, src, s in (("HI", "Id", 0.5), ("MI", "Id", -1.0), ("I8K", "Id", BIG), ("NHI", "Id", -0.5), ("I64", "Id", 64.0), ("NB", "B", -1.0),
+                         ("B8K", "B", BIG), ("NB8K", "B", -BIG), ("NB128", "B", -128.0)):
+        act(ref(name), ref(src), AF.Copy, scale=s)
+    keep_where(ref("L"), B, [[1, 128]], A.is_gt, 0.0, -1)
+    keep_where(ref("G"), B, [[-1, 128]], A.is_gt, 0.0, 1)
+    iota(ref("i64"), [[1, 64]], 0, 0)
+    iota(ref("ci"), [[16, 24]], -2048 - K, 0)
+    iota(ref("sbi", p=64), [[0, 512]], 63, 1)
+    iota(ref("rs0"), [[0, K]], 0, 0)
+    iota(ref("mk0", p=16), [[0, K]], -8192, 0)
+    keep_where(ref("SEL", p=64), ref("sbi", p=64), [[-16, 4], [0, 8], [-1, 16]], A.is_equal, 0.0, 1)
+    keep_where(ref("rs"), ref("rs0"), [[0, 24], [1, 16]], A.not_equal, -2.0 ** 31, 0)
+    keep_where(ref("mk", p=16), ref("mk0", p=16), [[0, 24], [-1, 16]], A.is_equal, -2.0 ** 30, 1)
+    keep_where(ref("EQ", p=16), ref("one", p=16), [[0, 8], [-1, 16]], A.is_equal, 0.0, 1)
 
-    def more_constants():
-        for name, src, s in (("MI", "Id", -1.0), ("NI16", "Id", -16.0),
-                             ("I14", "Id", 2.0 ** -14), ("FLM", "B", 2.0 ** 18), ("B64", "B", 64.0), ("PH", "B8", 0.5), ("MH", "B8", -0.5)):
-            act(ref(name), ref(src), AF.Copy, scale=s)
-        act(ref("CN"), ref("CK"), AF.Copy, scale=-1.0)
-
-    def picks(mat, scale):
-        act(ref(mat), ref("wr3"), AF.Copy, scale=0.0)
-        for r in range(16):
-            act(ref(mat, 129 * r, 128 * r + 128, 16), ref("B8"), AF.Copy, scale=ref(scale, r, r + 1))
-
-    def v_constants():
-        ts(ref("up"), ref("cl"), col(PL), A.is_gt)
+    def constants_v():
+        ts(ref("WF"), ref("L"), -64.0, A.mult)
+        ts(ref("G"), ref("G"), -1.0 / 32, A.mult)
         ts(ref("pj", 2, 3), ref("thi"), 4, A.arith_shift_right)
         ts(ref("pj", 3, 4), ref("thi"), 15, A.bitwise_and)
-        ts(col(THR), col(PL), 0.0, A.not_equal)
-        tt(ref("L"), ref("up"), B, A.mult)
-        ts(ref("WR"), ref("wr3"), col(PG), A.is_equal)
+        cp(col(TH), ref("thi"))
+        tt(ref("WF"), ref("WF"), ref("HI"), A.add)
         cp(ref("col", THA, THA + 2), ref("pj", 2, 4))
-        ts(ref("Lm"), ref("L"), -128.0, A.mult)
-        tt(ref("Gm"), ref("BmI"), ref("L"), A.subtract)
-        ts(col(PLM), col(PL), -1.0, A.mult, 3072.0, A.add)
-        ts(col(C_FAM), col(THA), -16.0, A.mult)
-        ts(col(C_FBM), col(THB), -1.0, A.mult)
-        tt(ref("Wv0"), ref("Lm"), Id, A.add)
-        ts(ref("Gm"), ref("Gm"), 2.0 ** -14, A.mult)
-        ts(col(C_WA), col(THA), -16.0, A.mult, 4096.0, A.add)
-        ts(ref("FAm"), B, col(C_FAM), A.mult, 64.0, A.mult)
-        ts(ref("FBm"), B, col(C_FBM), A.mult, 64.0, A.mult)
-        tt(ref("Wv0", 0, 128, 16), ref("Wv0", 0, 128, 16), ref("Gm", 0, 128, 16), A.subtract)
-        ts(ref("WFA"), ref("B8"), col(C_WA), A.mult)
-        ts(ref("WFB"), ref("B8"), col(C_FBM), A.mult)
+        for t in range(VIS):
+            cp(ref("Wv%d" % t), ref("WF"))
+        for t in range(VIS):
+            tt(ref("Wv%d" % t, t, 128, 16), ref("WF", t, 128, 16), ref("G", t, 128, 16), A.add)
 
-    def late_constants():
-        for t in range(1, VIS):
-            tt(ref("Wv%d" % t), ref("Lm"), Id, A.add)
-            ts(col(THR + t), col(PL), float(t), A.not_equal)
-        ts(ref("SEL", p=64), ref("sbi", p=64), ref("col", PP, PP + 1, p=64), A.is_equal)
-        for t in range(1, VIS):
-            w = ref("Wv%d" % t, t, 128, 16)
-            tt(w, w, ref("Gm", t, 128, 16), A.subtract)
-        ts(ref("cim"), ref("ci"), col(PL), A.add)
-        ts(ref("ge"), ref("cl", 0, 16), col(PL), A.is_le, -65536.0, A.mult)
+    def constants_s():
+        act(ref("Z", 15, 128, 16), ref("B8"), AF.Copy)
+        act(ref("WX"), ref("WF"), AF.Copy, scale=128.0)
+        act(ref("BmI8K"), ref("BmI"), AF.Copy, scale=BIG)
+        act(col(C_WA), col(THA), AF.Identity, scale=-16.0 / BIG, bias=4096.0 / BIG)
+        act(col(C_WB), col(THB), AF.Copy, scale=-1.0 / BIG)
+        act(col(BZ), col(TH), AF.Identity, scale=-BIG, bias=(1.0 - BIG) * BIG)
+        for name, j, s in (("PP", 0, 0.5), ("PP", 8, 0.5), ("PM", 0, 0.5), ("PM", 8, -0.5)):
+            act(ref(name, j, j + 8), ref("B8"), AF.Copy, scale=s)
+        for t in range(VIS):
+            act(col(THR + t), ref("eq", t, t + 1), AF.Identity, scale=-0.5 + (14 - t) / 32.0, bias=col(THB0))
+        act(ref("WFA"), ref("B8"), AF.Copy, scale=col(C_WA))
+        act(ref("WFB"), ref("B8"), AF.Copy, scale=col(C_WB))
+        act(ref("cim"), ref("ci"), AF.Identity, bias=col(PL))
 
-    def full(b, n=K):
-        return ref("b%d" % b, 0, n)
+    def bk(b, lo=0, hi=K, p=128):
+        return ref("b%d" % b, lo, hi, p=p)
 
-    def wrap(out, mat, src, first, last):
-        for r in range(16):
-            mm(out, ref(mat, 128 * r, 128 * r + 128), ref(src, r, K, 16), first and r == 0, last and r == 15)
+    def blk(name, c):
+        return ref(name, CH * c, CH * c + CH)
 
-    lexw, mngw = ref("lx", 0, W), ref("mn", 0, W)
+    def wrap(out, src, lo, hi, first=True, last=True):
+        group(out, [(ref("Z", 15 - r, 143 - r), ref(src, lo + r, hi, 16)) for r in range(16)], first, last)
 
-    def spread(t, b, on_v):
-        i0, i1 = BLK[b]
-        for k in range(16):
-            o, s = ref("X16", 16 * i0 + k, 16 * i1, 16), ref("x%d" % t, i0, i1)
+    HS, HU = (5, 2, 7), (3, 1, 0)
+
+    def hash_sums(t, c):
+        xs = blk("x%d" % t, c)
+        mm(bk(HS[c], 0, CH), ref("Wa"), xs, True, True)
+        mm(bk(HS[c], CH, 2 * CH), ref("Wb"), xs, True, True)
+        group(bk(HU[c], 0, CH), [("C6", ref("one")), ("Wa", xs)], True, False)
+        act(ref("Mh", 2 * CH * c, 2 * CH * (c + 1)), bk(HS[c], 0, 2 * CH), AF.Identity, bias=192.0 - 4095.0 / 8192.0, scale=1.0 / 4096.0)
+
+    def hash_rests(t, c):
+        e = 2 * CH * c
+        group(bk(HS[c], 2 * CH, 3 * CH), [("Wb", blk("x%d" % t, c)), ("NI4", ref("Mh", e + CH, e + 2 * CH))])
+        mm(bk(HU[c], 0, CH), ref("NI4"), ref("Mh", e, e + CH), False, True)
+        act(blk("UP", c), bk(HS[c], 2 * CH, 3 * CH), AF.Identity, bias=786432.0)
+
+    def hash_step(c, j):
+        u = bk(HU[c], 0, CH)
+        if j == 0:
+            tt(blk("pr", c), blk("UP", c), u, A.mult)
+        elif j == 1:
+            ts(blk("ps", c), blk("pr", c), 5, A.arith_shift_right)
+        elif j == 2:
+            tt(blk("pt", c), blk("ps", c), u, A.add)
+        elif j == 3:
+            ts(blk("hi", c), blk("pt", c), 4095, A.bitwise_and)
+        else:
+            cp(blk("hu", c), blk("hi", c))
+
+    def spread(t, on_v, ks):
+        for k in ks:
+            o, s = ref("X16", k, 16 * CH, 16), blk("x%d" % t, 0)
             if on_v:
                 cp(o, s)
             else:
                 act(o, s, AF.Copy)
 
-    def hash_s(t, b):
-        hash_1(t, b)
-        hash_2(b)
-        hash_3(b)
+    def hash_front(t):
+        def between(j):
+            spread(t, t == 0, (range(0, 4), range(4, 10), range(10, 16))[j])
+            if t == 0:
+                for k in (range(0, 6), range(6, 12), range(12, 16))[j]:
+                    act(ref("CK", 129 * k, 128 * k + 128, 16), ref("B8"), AF.Copy, scale=ref("cw", k, k + 1))
+        for c in (1, 0):
+            hash_sums(t, c)
+        between(0)
+        for c in (1, 0):
+            hash_rests(t, c)
+        hash_sums(t, 2)
+        between(1)
+        hash_rests(t, 2)
+        between(2)
 
-    def hash_1(t, b):
-        i0, i1 = HBL[b]
-        n = i1 - i0
-        xs = ref("x%d" % t, i0, i1)
-        mm(ref("b0", 0, n), ref("Wa"), xs, True, True)
-        mm(ref("b0", n, 2 * n), ref("Wb"), xs, True, True)
-        mm(full(2, n), ref("Wb"), xs, True, False)
-        mm(full(1, n), ref("C6"), ref("one", 0, n), True, False)
-        mm(full(1, n), ref("Wa"), xs, False, False)
+    SB, VB, XBK, HFB, TAB = (0, 2, 6), (1, 3, 7), 4, 5, 7
+    PIECES = (0, 26, 52, 78, 104, 128)
 
-    def hash_2(b):
-        n = HBL[b][1] - HBL[b][0]
-        act(ref("Mh", 0, 2 * n), ref("b0", 0, 2 * n), AF.Identity, bias=192.0 - 4095.0 / 8192.0, scale=1.0 / 4096.0)
-
-    def hash_3(b):
-        n = HBL[b][1] - HBL[b][0]
-        mm(full(2, n), ref("NI4"), ref("Mh", n, 2 * n), False, True)
-        mm(full(1, n), ref("NI4"), ref("Mh", 0, n), False, True)
-        act(ref("UP", 0, n), full(2, n), AF.Identity, bias=786432.0)
-
-    def hash_v(b):
-        i0, i1 = HBL[b]
-        n = i1 - i0
-        hv = [(0, n // 2), (n // 2, n)]
-        for a, e in hv:
-            tt(ref("pr", a, e), ref("UP", a, e), ref("b1", a, e), A.mult)
-        for a, e in hv:
-            ts(ref("ps", a, e), ref("pr", a, e), 5, A.arith_shift_right)
-        for a, e in hv:
-            tt(ref("pt", a, e), ref("ps", a, e), ref("b1", a, e), A.add)
-        for a, e in hv:
-            ts(ref("hi", i0 + a, i0 + e), ref("pt", a, e), 4095, A.bitwise_and)
-        for a, e in hv:
-            cp(ref("hu", i0 + a, i0 + e), ref("hi", i0 + a, i0 + e))
-
-    def pick(i0, i1):
+    def look_v(i0, i1):
         tt(ref("D", 16 * i0, 16 * i1), ind(lexw, ref("hu", i0, i1)), ref("X16", 16 * i0, 16 * i1), A.not_equal)
 
-    def count(b):
-        i0, i1 = BLK[b]
+    def look_s(i0, i1):
+        act(ref("C", 16 * i0, 16 * i1), ind(lexw, ref("hu", i0, i1)), AF.Copy)
+
+    def compare(i0, i1):
         for k in range(16):
-            mm(ref("b3", i0, i1), ref("CK", 128 * k, 128 * k + 128), ref("D", 16 * i0 + k, 16 * i1, 16), k == 0, k == 15)
+            tt(ref("D", 16 * i0 + k, 16 * i1, 16), ref("C", 16 * i0 + k, 16 * i1, 16), bk(XBK, i0, i1), A.not_equal)
 
-    def look_s(t, b):
-        i0, i1 = BLK[b]
-        n = i1 - i0
-        w, o = lexw, ref("hu", i0, i1)
-        do("s", lambda: g.scalar.activation(ref("C")[3], w[3].indirect(o[3]), AF.Copy), [w, o], [ref("C")])
-        for h in range(2):
-            for k in range(8):
-                c = ref("b%d" % (6 + h), n * k, n * k + n)
-                mm(c, ref("MI"), ref("x%d" % t, i0, i1), True, False)
-                mm(c, Id, ref("C", 8 * h + k, 1024, 16), False, True)
+    def count(i0, i1):
+        c = i0 // CH
+        group(bk(SB[c], i0 - CH * c, i1 - CH * c), [(ref("CK", 128 * k, 128 * k + 128), ref("D", 16 * i0 + k, 16 * i1, 16)) for k in range(16)])
 
-    def unlike_s():
-        for h in range(2):
-            act(ref("CA", 512 * h, 512 * h + 512), full(6 + h, 512), AF.Abs)
-        act(ref("C"), ref("CA"), AF.Relu, bias=1.0, scale=-1.0)
+    def pairs(c):
+        act(blk("pm", c), bk(SB[c], 0, CH), AF.Sign, bias=-13.5, scale=-1.0)
 
-    def count_s(b):
-        i0, i1 = BLK[b]
-        n = i1 - i0
-        mm(ref("b3", i0, i1), ref("one", 0, 128), ref("neg", 0, n), True, False)
-        for h in range(2):
-            for k in range(8):
-                j = 8 * h + k
-                mm(ref("b3", i0, i1), ref("CN", 128 * j, 128 * j + 128), ref("C", n * j, n * j + n), False, j == 15)
+    def lowest(t, c):
+        pm = blk("pm", c)
+        mm(bk(VB[c], 0, CH), ref("Wv%d" % t), pm, True, True)
+        group(bk(SB[c], 2 * CH, 3 * CH), [("Id", blk("x%d" % t, c)), ("WX", pm)])
+        mm(bk(SB[c], CH, 2 * CH), ref("WF"), pm, True, True)
 
-    def scatter(buf, src):
-        w, o, s = ref(buf), ref("lo"), ref(src)
+    def pair_lane(c):
+        act(blk("Fx", c), bk(SB[c], 2 * CH, 3 * CH), AF.Relu, bias=col(BFX))
+        act(blk("Fm", c), bk(SB[c], CH, 2 * CH), AF.Relu, bias=col(BF8), scale=BIG)
+
+    def lane(t, c):
+        ts(blk("Le", c), bk(VB[c], 0, CH), col(THR + t), A.is_ge)
+
+    def place(c):
+        tt(blk("Lh", c), blk("Le", c), bk(HFB, CH * c, CH * c + CH), A.mult)
+
+    def place_wrap(c):
+        wrap(bk(VB[c], CH, CH + 8), "Lh", CH * c, CH * c + CH)
+
+    def place_list(c):
+        ts(ref("le", 8 * c, 8 * c + 8), bk(VB[c], CH, CH + 8), 2048.0, A.add)
+
+    def letters(c):
+        tt(blk("LC", c), ind(lexw, ref("le", 8 * c, 8 * c + 8)), blk("Le", c), A.mult)
+
+    def meanings(t, c):
+        tt(blk("d", c), ind(mngw, ref("le", 8 * c, 8 * c + 8)), blk("m%d" % t, c), A.subtract)
+
+    def distance(c):
+        act(blk("ad", c), blk("d", c), AF.Abs)
+
+    def by_words_t(c):
+        group(bk(SB[c], 392, 408), [(blk("Fx", c), ref("PP")), (blk("LC", c), ref("PM"))])
+        group(bk(SB[c], 384, 392), [(blk("Fm", c), ref("WFA")), (blk("Fm", c), ref("WFB")), (blk("ad", c), ref("B8"))])
+        group(bk(SB[c], 0, CH), [("Id", blk("Fm", c)), ("B", blk("ad", c))])
+
+    def by_words_s(c):
+        act(ref("mr", 16 * c, 16 * c + 16), bk(SB[c], 392, 408), AF.Abs, bias=-32.0)
+        act(ref("nf", 8 * c, 8 * c + 8), bk(SB[c], 384, 392), AF.Relu, bias=-4095.0)
+
+    def rows_s(c):
+        for j in range(8):
+            q = 8 * c + j
+            act(ref("ab", 64 * q, 64 * q + 64), ref("i64"), AF.Abs, bias=ref("mr", 16 * c + j, 16 * c + j + 1), scale=-1.0)
+
+    def rows_v(c):
+        for j in range(8):
+            q = 8 * c + j
+            u = ref("U", 64 * q, 64 * q + 64)
+            ts(u, ref("ab", 64 * q, 64 * q + 64), ref("mr", 16 * c + 8 + j, 16 * c + 9 + j), A.is_equal, ref("nf", q, q + 1), A.mult)
+
+    def rows_t(c):
+        for j in range(8):
+            q = 8 * c + j
+            u = ref("U", 64 * q, 64 * q + 64)
+            mm(bk(TAB, 0, 64, p=64), u, u, q == 0, q == 23)
+
+    def side_t(t, c):
+        group(bk(SB[c], CH, 2 * CH), [("B", blk("Fx", c))])
+        group(bk(SB[c], 2 * CH, 3 * CH), [("Id", blk("x%d" % t, c)), ("I8K", blk("Le", c)), ("MI", blk("Fm", c))])
+
+    def side_s(c):
+        act(blk("Xf", c), bk(SB[c], CH, 2 * CH), AF.Identity, bias=-1.0)
+        act(blk("xp", c), bk(SB[c], 2 * CH, 3 * CH), AF.Copy)
+
+    def not_free(c):
+        act(blk("Zf", c), bk(SB[c], 0, CH), AF.Relu, bias=col(BZ), scale=BIG)
+
+    WB, Z1, MB, DB, S1, GB, Z2 = 4, 5, 2, 3, 1, 7, (0, 6, 4)
+
+    def same_place(c):
+        mm(bk(Z2[c], 0, CH), ref("NB8K"), blk("O", c), False, False)
+        for j in range(7):
+            q = 8 * c + j
+            i0, i1 = 16 * q + 16, CH * (c + 1)
+            e = ref("E", CH * q, CH * q + i1 - i0)
+            ts(e, ref("Hb", i0, i1), bk(S1, 16 * q + 15, 16 * q + 16), A.is_equal)
+            mm(bk(Z2[c], i0 - CH * c, CH), ref("NB8K"), e, False, j == 6)
+
+    def writers(c):
+        scan(blk("sj", c), ref("rs", 0, CH), bk(Z2[c], 0, CH), A.add, A.max)
+
+    def writers_places(c):
+        tt(ref("z", 8 * c, 8 * c + 8), ref("sj", CH * c + 15, CH * c + CH, 16), ref("cim", 8 * c, 8 * c + 8), A.max)
+
+    def writers_list(c):
+        ts(ref("lo", 8 * c, 8 * c + 8), ref("z", 8 * c, 8 * c + 8), 2048.0 + K, A.add)
+
+    def scatter(buf, src, c):
+        w, o, s = ref(buf), ref("lo", 8 * c, 8 * c + 8), blk(src, c)
         do("v", lambda: g.vector.tensor_copy(w[3].indirect(o[3]), s[3]), [o, s], [w])
 
-    hash_s(0, 0)
-    spread(0, 0, True)
-    hash_v(0)
+    hash_front(0)
+    constants_v()
+    constants_s()
+    for j in range(5):
+        for c in (1, 0):
+            hash_step(c, j)
     for t in range(VIS):
         x, m, last = "x%d" % t, "m%d" % t, t == VIS - 1
         xn, gn = "xn%d" % t, "gn%d" % t
         to = (rank + 2) % N if last else (rank - 1) % N
 
-        hash_s(t, 1)
-        i0, i1 = HBL[1]
-        n = i1 - i0
-        pick(0, 32)
-        tt(ref("pr", 0, n), ref("UP", 0, n), full(1, n), A.mult)
-        pick(32, 64)
-        ts(ref("ps", 0, n), ref("pr", 0, n), 5, A.arith_shift_right)
-        pick(64, 96)
-        tt(ref("pt", 0, n), ref("ps", 0, n), full(1, n), A.add)
-        pick(96, 128)
-        ts(ref("hi", i0, i1), ref("pt", 0, n), 4095, A.bitwise_and)
-        ts(full(5, i0), ref("hi", 0, i0), -2048.0, A.add)
-        cp(ref("hu", i0, i1), ref("hi", i0, i1))
-        count(0)
-        spread(t, 1, False)
-        if t == 0:
-            more_constants()
-        look_s(t, 3)
-        spread(t, 2, False)
-        unlike_s()
-        act(full(4), ref(x), AF.Copy)
-        pick(*BLK[1])
-        count(1)
-        count_s(3)
-        pick(*BLK[2])
-        count(2)
-        if t == 0:
-            v_constants()
-            picks("WI", "eq")
-        ts(ref("b5", i0, i1), ref("hi", i0, i1), -2048.0, A.add)
-        if t > 0:
-            scatter("mn", "gn%d" % (t - 1))
+        def old_meanings(c):
+            if t > 0:
+                scatter("mn", "gn%d" % (t - 1), c)
 
-        ts(ref("pm"), full(3), -13.5, A.is_le)
-        mm(full(0), ref("Wv%d" % t), ref("pm"), True, True)
-        halves = [(0, K // 2), (K // 2, K)]
-        for a, e in halves:
-            ts(ref("Le", a, e), ref("b0", a, e), col(THR + t), A.is_ge)
-        act(ref("nb"), full(0), AF.Abs, bias=col(THR + t))
-        act(ref("Fm"), full(0), AF.Relu)
-        for a, e in halves:
-            tt(ref("Lh", a, e), ref("Le", a, e), ref("b5", a, e), A.mult)
-        tt(ref("Lx"), ref("Le"), full(4), A.mult)
-        wl = ref("b2", 0, 24)
-        wrap(wl, "WR", "Lh", True, True)
-        mm(full(1), B, ref("Lx"), True, True)
-        act(ref("NP"), ref("nb"), AF.Relu, bias=64.0, scale=-2.0 ** 20)
-        ts(ref("le"), wl, 2048.0, A.add)
-        ts(ref("hw"), wl, -16384.0, A.add)
-        act(ref("XB"), full(1), AF.Identity, bias=192.0 - 15.0 / 32.0, scale=1.0 / 16.0)
-        wm = ref("b2", 0, 24)
-        mm(wm, B, ref("zz", 0, 24), True, False)
-        for c in range(3):
-            o, fc = ref("b2", 8 * c, 8 * c + 8), ref("Fm", 128 * c, 128 * c + 128)
-            mm(o, fc, ref("WFA"), False, False)
-            mm(o, fc, ref("WFB"), False, False)
-        mm(ref("b3", 0, 48), B, ref("zz"), True, False)
-        for c in range(3):
-            lxc = ref("Lx", 128 * c, 128 * c + 128)
-            mm(ref("b3", 8 * c, 8 * c + 8), lxc, ref("MH"), False, False)
-            mm(ref("b3", 24 + 8 * c, 32 + 8 * c), lxc, ref("PH"), False, False)
-        mm(full(6), Id, ref("Lx"), True, False)
-        mm(full(6), Id, ref("NP"), False, True)
-        mm(full(0), Id, ref(x), True, False)
-        mm(full(0), ref("MI"), ref("NP"), False, True)
+        look_s(128, 192)
+        look_s(192, 256)
+        mm(bk(XBK), Id, ref(x), True, True)
+        for j in range(5):
+            hash_step(2, j)
+            look_v(PIECES[j], PIECES[j + 1])
+        look_s(256, 320)
+        look_s(320, 384)
+        ts(ref("hf"), ref("hu"), -2048.0, A.add)
+        count(0, 128)
+        mm(bk(HFB), Id, ref("hf"), True, True)
+        for i in (128, 192, 256):
+            compare(i, i + 64)
+            count(i, i + 64)
+        for c in (0, 1):
+            pairs(c)
+        for c in (0, 1):
+            lowest(t, c)
+        compare(320, 384)
+        count(320, 384)
 
-        tt(ref("d"), ind(mngw, ref("le")), ref(m), A.subtract)
-        act(ref("ad"), ref("d"), AF.Abs)
-        tt(ref("LC"), ind(lexw, ref("le")), ref("Le"), A.mult)
-        act(ref("XC"), ref("XB"), AF.Copy, scale=64.0)
-        if t == 0:
-            late_constants()
-        wl2 = ref("b7", 0, 24)
+        for c in (0, 1):
+            pair_lane(c)
+        for c in (0, 1):
+            lane(t, c)
+        for c in (0, 1):
+            place(c)
+        pairs(2)
+        place_wrap(0)
+        lowest(t, 2)
+        place_wrap(1)
+        old_meanings(2)
+        place_list(0)
+        old_meanings(1)
+        lane(t, 2)
+        pair_lane(2)
+        old_meanings(0)
+        place(2)
+        for c in (0, 1):
+            side_t(t, c)
+        place_wrap(2)
+        meanings(t, 0)
+        place_list(1)
+        letters(0)
+        side_s(0)
+        side_s(1)
+        distance(0)
+        meanings(t, 1)
+        by_words_t(0)
+        place_list(2)
+        letters(1)
+        distance(1)
+        by_words_s(0)
+        meanings(t, 2)
+        letters(2)
+        by_words_t(1)
+        side_t(t, 2)
+        pw, lfw = bk(VB[1], 2 * CH, 2 * CH + 24), bk(VB[0], 2 * CH, 2 * CH + 24)
+        wrap(pw, "Fx", 0, K)
+        rows_s(0)
+        distance(2)
+        by_words_t(2)
+        by_words_s(1)
+        rows_v(0)
+        rows_s(1)
+        by_words_s(2)
+        rows_t(0)
+        wrap(lfw, "LC", 0, K, True, False)
+        rows_v(1)
+        rows_s(2)
+        act(ref("XB"), pw, AF.Identity, bias=128.0 - 15.0 / 32, scale=1.0 / 16)
+        rows_t(1)
+        rows_v(2)
+        rows_t(2)
+        mm(lfw, ref("I64"), ref("XB"), False, True)
+        mm(bk(DB), B, ref("Lh"), True, True)
+        side_s(2)
         for c in range(3):
-            mm(ref("b2", 8 * c, 8 * c + 8), ref("ad", 128 * c, 128 * c + 128), ref("B8"), False, c == 2)
-        for c in range(3):
-            lcc = ref("LC", 128 * c, 128 * c + 128)
-            mm(ref("b3", 8 * c, 8 * c + 8), lcc, ref("MH"), False, False)
-            mm(ref("b3", 24 + 8 * c, 32 + 8 * c), lcc, ref("MH"), False, c == 2)
-        act(ref("mc"), ref("b3", 0, 24), AF.Copy)
-        act(ref("rc"), ref("b3", 24, 48), AF.Abs)
-        ts(ref("hd"), ref("d"), 0.5, A.mult, -0.25, A.add)
-        tt(ref("LCm"), ref("LC"), full(6), A.min)
-        ts(ref("nf"), ref("b2", 0, 24), 4095.5, A.is_ge)
-        wrap(wl2, "WI", "XC", True, False)
-        for q in range(24):
-            act(ref("ab", 64 * q, 64 * q + 64), ref("i64"), AF.Abs, bias=ref("mc", q, q + 1))
+            not_free(c)
+        act(ref("ha"), ref("ad"), AF.Identity, bias=127.8, scale=0.5)
 
-        for q in range(24):
-            u = ref("U", 64 * q, 64 * q + 64)
-            ts(u, ref("ab", 64 * q, 64 * q + 64), ref("rc", q, q + 1), A.is_equal, ref("nf", q, q + 1), A.mult)
-            mm(ref("b1", 0, 64, p=64), u, u, q == 0, q == 23)
-            if q == 7:
-                mm(full(6), B, ref("Lx"), True, False)
-                mm(full(6), ref("NI16"), ref("XB"), False, True)
-        act(ref("XT"), full(0), AF.Copy)
-        act(ref("la"), full(6), AF.Abs, bias=col(PLM))
-        wrap(wl2, "WR", "LC", False, True)
-        ts(ref("TS", p=64), ref("b1", 0, 64, p=64), 1.0, A.min)
-        ts(ref("lf"), wl2, -12288.0, A.add)
+        ts(ref("TS", p=64), bk(TAB, 0, 64, p=64), 1.0, A.min)
+        ts(ref("lf"), lfw, -64.0 * 132, A.add)
         for b in range(4):
-            mm(ref("b2", 64 * b, 64 * b + 64), ref("SEL", 128 * b, 128 * b + 128, p=64), ref("TS", p=64), True, True)
-        act(ref("lh"), ref("la"), AF.Relu, bias=1.0, scale=-1.0)
-        if t == 0:
-            picks("WG", "ge")
-        mm(full(3), B, ref("Lh"), True, True)
-        for lw, src in (("B64", "Le"), ("FAm", "Fm"), ("FBm", "Fm"), ("B64", "ad")):
-            mm(full(5), ref(lw), ref(src), src == "Le", False)
-        cp(ref("TW"), ref("b2", 0, 256))
-        tt(ref("RF"), ind(ref("TW"), ref("lf")), ref("lh"), A.mult)
-        cp(ref("Hb"), full(3))
-        mm(full(5), ref("FLM"), ref("RF"), False, True)
-        mm(full(4), Id, ref(x), True, False)
-        mm(full(4), ref("MI"), ref("Lx"), False, False)
-        mm(full(4), Id, ref("LCm"), False, True)
-        wl3 = ref("b2", 0, 24)
-        mm(full(6), Id, ref(m), True, False)
+            mm(bk(TAB, 64 + 64 * b, 128 + 64 * b), ref("SEL", 128 * b, 128 * b + 128, p=64), ref("TS", p=64), True, True)
+        cp(ref("Hb"), bk(DB))
+        cp(ref("TW"), bk(TAB, 64, 320))
+        group(bk(WB), [("Id", ref("LC")), ("BmI8K", ref("Le")), ("B", ref("Zf"))], True, False)
+        group(bk(Z1), [(ref("EQ", p=16), ref("mk", p=16)), ("B", ref("Lh")), ("B", ref("Fm")), ("NB", ref("Zf"))], True, False)
+        group(bk(MB), [("B", ref("Fm")), ("NB", ref("Zf"))], True, False)
+        tt(ref("RF"), ind(ref("TW"), ref("lf")), ref("Xf"), A.is_equal)
+        mm(bk(WB), ref("B8K"), ref("RF"), False, True)
+        mm(bk(Z1), ref("NB8K"), ref("RF"), False, True)
+        mm(bk(MB), ref("NB8K"), ref("RF"), False, True)
+        group(bk(DB), [("HI", ref("d")), ("NHI", ref("ad")), ("Id", ref("ha")), ("NB128", ref("Le"))])
 
-        ts(ref("M"), full(5), 32.0, A.is_lt, 16384.0, A.mult)
-        wrap(wl3, "WI", "M", True, True)
-        act(full(1), ref("M"), AF.Copy)
-        for a, e in halves:
-            tt(ref("tx", a, e), ref("XT", a, e), ref("b5", a, e), A.min)
-        for a, e in halves:
-            tt(ref(xn, a, e), ref("tx", a, e), ref("b4", a, e), A.max)
+        tt(ref(xn), ref("xp"), bk(WB), A.min)
         send(ref(xn), ref("x%d" % (t + 1)), to, "ax%d" % (t + 1))
-        tt(ref("hp"), ref("hw"), wl3, A.add)
-        ts(ref("z3"), wl3, -2.0, A.mult, 34816.0, A.add)
-        for q in range(24):
-            n, e = K - 16 * q, 384 * q
-            ts(ref("E", e, e + n), ref("Hb", 16 * q, K), ref("hp", q, q + 1), A.is_equal)
-            mm(ref("b7", 16 * q, K), B, ref("E", e, e + n), q == 0, q == 23)
-            if q == 5:
-                tt(ref("z3"), ref("z3"), ref("hp"), A.add)
-            if q == 8:
-                tt(ref("gd"), ref("hd"), full(1), A.mult)
-            if q == 11:
-                tt(ref("z"), ref("z3"), ref("cim"), A.min)
-        act(ref("LB"), full(7), AF.Copy, scale=65536.0)
-        wl4 = ref("b5", 0, 24)
-        for r in range(16):
-            mm(wl4, ref("WG", 128 * r, 128 * r + 128), ref("E", r, 24 * K, K), r == 0, False)
-        wrap(wl4, "WI", "LB", False, True)
-        mm(full(6), ref("I14"), ref("gd"), False, True)
-        act(ref(gn), full(6), AF.Copy)
+        act(ref("M"), bk(MB), AF.Relu, scale=1.0 / BIG)
+        scan(bk(S1), ref("rs"), bk(Z1), A.add, A.max)
+        mm(bk(GB), Id, ref(m), True, False)
+        for c in (2, 1, 0):
+            group(bk(Z2[c], 0, CH), [(ref("EQ", p=16), ref("mk", 0, CH, p=16)), ("B", blk("Lh", c)), ("I8K", blk("M", c))], True, False)
+        tt(ref("O", 1, K), ref("Hb", 1, K), bk(S1, 0, K - 1), A.is_equal)
+        tt(ref("gd"), ref("M"), bk(DB), A.mult)
+        mm(bk(GB), Id, ref("gd"), False, True)
+        act(ref(gn), bk(GB), AF.Copy)
         send(ref(gn), ref("m%d" % (t + 1)), to, "ag%d" % (t + 1))
+        same_place(2)
+        same_place(1)
+        writers(2)
+        same_place(0)
+        writers_places(2)
+        writers(1)
+        writers_list(2)
+        writers_places(1)
+        writers(0)
         if not last:
-            hash_s(t + 1, 0)
-            spread(t + 1, 0, False)
-        tt(ref("z1"), ref("cim"), wl4, A.min)
-        tt(ref("z2"), ref("z1"), ref("z"), A.max)
-        cp(ref("lo"), ref("z2"))
-        scatter("lx", xn)
+            hash_front(t + 1)
+        scatter("lx", xn, 2)
+        writers_list(1)
+        writers_places(0)
+        scatter("lx", xn, 1)
+        writers_list(0)
         if last:
+            scatter("mn", gn, 2)
+            scatter("lx", xn, 0)
+            store("y", T.yx[:, :], ref("x3"), "ox")
             store("y", T.yl[:, :], lexw, "ol")
-            scatter("mn", gn)
+            store("y", T.yg[:, :], ref("m3"), "og")
+            scatter("mn", gn, 1)
+            scatter("mn", gn, 0)
         else:
-            hash_v(0)
+            for j in range(5):
+                for c in (1, 0):
+                    hash_step(c, j)
+                if j == 0:
+                    scatter("lx", xn, 0)
 
-    half = W // 2
-    act(ref("D", 0, half), ref("mn", 0, half), AF.Copy, accum=ref("ya"))
-    do("v", lambda: g.vector.tensor_reduce(ref("yb")[3], ref("mn", half, W)[3], AxisListType.X, A.add), [ref("mn", half, W)], [ref("yb")])
-    tt(ref("ya"), ref("ya"), ref("yb"), A.add)
-    store("y", T.yx[:, :], ref("x3"), "ox")
-    store("y", T.yg[:, :], ref("m3"), "og")
-    store("y", T.ym[:, :], ref("ya"), "om")
+    act(ref("D", 0, W - 2 * SUMV), ref("mn", K + 2 * SUMV, K + W), AF.Copy, accum=ref("ya"))
+    scan(ref("run"), ref("mn", K, K + SUMV), ref("mn", K + SUMV, K + 2 * SUMV), A.add, A.add)
+    tt(ref("yb"), ref("ya"), ref("run", SUMV - 1, SUMV), A.add)
+    store("y", T.ym[:, :], ref("yb"), "om")
     for q in ("v", "s", "t", "g"):
         g.wait_ge(T.sem[own[q]], cnt[q])
     g.wait_ge(T.sem["rl"], sent[0])

@@ -3,38 +3,54 @@ from concourse.mybir import dt, AluOpType, AxisListType, ActivationFunctionType
 N, W, K, VIS = 6, 4096, 384, 3
 CH = 128
 NENG = 8
-SUMV = 1408
 BF, F32, I32, U16, F16 = "bfloat16", "float32", "int32", "uint16", "float16"
 SCRATCH = {
     "lx": ("sbuf", [128, K + W], BF), "mn": ("sbuf", [128, K + W], BF),
     "wti": ("sbuf", [128, 2], I32), "thi": ("sbuf", [128, 1], I32), "pi": ("sbuf", [128, 1], I32), "pj": ("sbuf", [128, 4], I32),
     "col": ("sbuf", [128, 24], F32), "i64": ("sbuf", [128, 64], BF), "one": ("sbuf", [128, 128], BF),
-    "X16": ("sbuf", [128, 16 * CH], BF), "C": ("sbuf", [128, 16 * K], BF), "D": ("sbuf", [128, 16 * K], BF), "E": ("sbuf", [128, 24 * CH], BF),
+    "X16": ("sbuf", [128, 16 * CH], BF), "C": ("sbuf", [128, 16 * K], BF), "D": ("sbuf", [128, 16 * K], BF), "E": ("sbuf", [128, 24, CH], BF),
     "UP": ("sbuf", [128, K], F32), "Mh": ("sbuf", [128, 2 * K], BF),
     "hu": ("sbuf", [128, K], U16), "hf": ("sbuf", [128, K], F16), "Lh": ("sbuf", [128, K], F16), "Hb": ("sbuf", [128, K], F16),
     "le": ("sbuf", [128, 24], U16), "lf": ("sbuf", [128, 24], U16), "lo": ("sbuf", [128, 24], U16),
     "ab": ("sbuf", [128, 1536], BF), "U": ("sbuf", [128, 1536], BF), "TS": ("sbuf", [128, 64], BF), "TW": ("sbuf", [128, 256], BF),
-    "ya": ("sbuf", [128, 1], F32), "yb": ("sbuf", [128, 1], F32), "CK": ("sbuf", [128, 2048], BF), "Z": ("sbuf", [128, 144], BF),
-    "mr": ("sbuf", [128, 48], F32), "XB": ("sbuf", [128, 24], BF), "PP": ("sbuf", [128, 16], BF), "PM": ("sbuf", [128, 16], BF),
-    "sj": ("sbuf", [128, K], F32), "run": ("sbuf", [128, SUMV], F32),
+    "ya": ("sbuf", [128, 5], F32), "yb": ("sbuf", [128, 1], F32), "CK": ("sbuf", [128, 2048], BF), "Z": ("sbuf", [128, 144], BF),
+    "mr": ("sbuf", [128, 48], F32), "XB": ("sbuf", [128, 24], BF), "CB": ("sbuf", [128, 24], BF), "FL": ("sbuf", [128, 2 * K], BF),
+    "PP": ("sbuf", [128, 16], BF), "PM": ("sbuf", [128, 16], BF), "sj": ("sbuf", [128, K], F32), "s1": ("sbuf", [128, K], F32),
 }
-for _n in ("x0 x1 x2 x3 m0 m1 m2 m3 xn0 xn1 xn2 gn0 gn1 gn2 pm Le Fm Fx d ad LC ha Zf Xf xp RF M gd O rs rs0 mk mk0").split():
+for _n in ("x0 x1 x2 x3 m0 m1 m2 m3 xn0 xn1 xn2 gn0 gn1 gn2 pm Le Fm d ad nd ha Zf Xf xp RF M gd df mk mk0").split():
     SCRATCH[_n] = ("sbuf", [128, K], BF)
-for _n in ("cg cl cq B Id BmI L G WF WX Wv0 Wv1 Wv2 Wa Wb C6 NI4 MI NB B8K NB8K I8K BmI8K HI NHI NB128 I64 EQ").split():
+for _n in ("cg cl cq B Id BmI L WF WX Wv0 Wv1 Wv2 Wa Wb Wc C6 C7 NI4 NI7 MI NB B8K NB8K NL8K I8K WL W7 B4K NB4K NB128 I64 EQ rs rs0 mj").split():
     SCRATCH[_n] = ("sbuf", [128, 128], BF)
-for _n in ("B8 WFA WFB").split():
+for _n in ("B8 G WFA WFB WFC WFD").split():
     SCRATCH[_n] = ("sbuf", [128, 8], BF)
 for _n in ("sbi SEL").split():
     SCRATCH[_n] = ("sbuf", [128, 512], BF)
-for _n in ("pr ps pt hi").split():
+for _n in ("pr pt hi").split():
     SCRATCH[_n] = ("sbuf", [128, K], I32)
 for _n in ("eq cw").split():
     SCRATCH[_n] = ("sbuf", [128, 16], F32)
-for _n in ("ci cim nf z").split():
+for _n in ("ci cim z zz").split():
     SCRATCH[_n] = ("sbuf", [128, 24], F32)
 for _b in range(8):
     SCRATCH["b%d" % _b] = ("psum", [128, 512], F32)
-SEMAPHORES = ["qv", "qs", "qt", "qg", "lx", "lw", "lt", "lg", "ll", "lm", "ax1", "ag1", "ax2", "ag2", "ax3", "ag3", "rl", "ox", "og", "ol", "om"]
+SIDE = {"Fx": 0, "LC": K}
+SEMAPHORES = ["qv", "qs", "qt", "qg", "lx", "lw", "lt", "lg", "ll", "lm", "ax1", "bx1", "ag1", "ax2", "bx2", "ag2", "ax3", "bx3", "ag3",
+              "rl", "ox", "og", "ol", "om"]
+ORDER = """look_s 128 192, look_s 192 256, look_v 0 24, hash 2 0, look_v 24 44, hash 2 1, look_v 44 64, hash 2 2, look_v 64 84, hash 2 3, look_s 256 320,
+look_v 84 128, places_v, words_t, count 0 64, compare 128 192, count 128 192, compare 192 256, count 64 128, places_t, count 192 256, look_s 320 384,
+compare 256 320, count 256 320, compare 320 384, pairs 0, lowest 0, narrow, lane_s 0, lane_s 1, count 320 384, pairs 1, pair_letter 0, pair_lane 0,
+lowest 1, pair_letter 1, pair_lane 1, old_meanings 1, place 0, place 1, place_wrap 0, pair_t 0, kept_t 0, pair_s 0, kept_s 0, old_meanings 0, lane 2,
+kept_t 1, place_list 0, place 2, letters 0, meanings 0, place_wrap 1, halves_t 0, meanings 1, distance 0, pair_t 1, free_t 0, place_list 1, letters 1,
+meanings 2, halves_s 0, distance 1, free_t 1, halves_t 1, rows_s 0, rows_v 0, rows_s 1, rows_v 1, code_wrap, far_t 0, halves_s 1, distance 2,
+free_t 2, rows_t 0, rows_t 1, rows_s 2, own_high, kept_s 1, code_low, rows_v 2, rows_t 2, table, code_high, code_list, far_t 1, not_free 0, all_t,
+all_v 2, all_v 1, found_t 1, table_t, table_v, half, sum_before 0, not_free 1, pair_s 1, below, sum_before 1, flagged 0, again_t, found_t 0,
+found_far 0, masked_t, merging_t 1, found_far 1, flagged 1, found_flag 0, merge_t 1, new_letters 0, send_letters 0, found_flag 1, new_letters 1,
+send_letters 1, merging_t 2, merge_t 2, merge, mergers 2, mergers 1, mergers 0, same_s 0, same_s 1, same_v 2, mean_t, mean_half, mean_v,
+places_again 0, places_again 1, places_again 2, new_t 0, same_t 2, new_t 1, new_meanings, keep, send_meanings, spread_g 11 16, same_v 1, writers 2,
+same_t 1, merged_again 2, writers 1, writers_places 2, merged_again 1, same_t 0, writers 0, writers_list 2, writers_places 1, merged_again 0, write 2,
+writers_list 1, writers_places 0, write 1, writers_list 0, sums 1, change 2, write 0, sums 0, floors 1, more 1, rests 1, floors 0, sum_before 2,
+rests 0, sum_before 3, spread_s 3 7, more 0, other 1, write_meanings 2, change 1, other 0, next 1 0, next 0 0, next 1 1, next 0 1, next 1 2, sums 2,
+changes, spread_s 0 3, floors 2, spread_s 7 11, next 0 2, write_meanings 1, sums_v, next 1 3, more 2, rests 2, other 2, change 0, next 0 3"""
 
 
 def rank_program(g, core, T, topo):
@@ -50,6 +66,8 @@ def rank_program(g, core, T, topo):
     acc = {}
 
     def ref(name, lo=0, hi=None, step=1, p=128):
+        if name in SIDE:
+            return ref("FL", SIDE[name] + lo, SIDE[name] + (K if hi is None else hi), step, p)
         hi = T[name].shape[1] if hi is None else hi
         return (name, lo, hi, T[name][0:p, lo:hi:step] if step != 1 else T[name][0:p, lo:hi], step)
 
@@ -133,8 +151,8 @@ def rank_program(g, core, T, topo):
     def fill(out, c):
         do("v", lambda: g.vector.memset(ap(out), c), [], rd(out))
 
-    def scan(out, a, b, op0, op1):
-        do("v", lambda: g.vector.tensor_tensor_scan(ap(out), ap(a), ap(b), 0.0, op0, op1), rd(a, b), rd(out))
+    def scan(out, a, b, op0, op1, first=0.0):
+        do("v", lambda: g.vector.tensor_tensor_scan(ap(out), ap(a), ap(b), ap(first), op0, op1), rd(a, b, first), rd(out))
 
     def act(out, a, f, bias=0.0, scale=1.0, accum=None):
         if accum is None:
@@ -155,8 +173,8 @@ def rank_program(g, core, T, topo):
         else:
             do("g", lambda: g.iota(ap(out), pattern, base, cm), [], rd(out))
 
-    def keep_where(out, a, pattern, op, other, cm):
-        do("g", lambda: g.affine_select(ap(out), ap(a), pattern, op, other, 0, cm), rd(a), rd(out))
+    def keep_where(out, a, pattern, op, other, cm, base=0):
+        do("g", lambda: g.affine_select(ap(out), ap(a), pattern, op, other, base, cm), rd(a), rd(out))
 
     def load(q, out, src, sem):
         Q[q].dma_start(ap(out), src).then_inc(T.sem[sem], 16)
@@ -188,19 +206,19 @@ def rank_program(g, core, T, topo):
     load("y", ref("thi"), T.th[:, :], "lt")
     load("s", mngw, T.mng[:, :], "lm")
     for t in (1, 2, 3):
-        note("ax%d" % t, NENG, None, [], [ref("x%d" % t)])
+        note("ax%d" % t, NENG, None, [], [ref("x%d" % t, 0, 2 * CH)])
+        note("bx%d" % t, NENG, None, [], [ref("x%d" % t, 2 * CH, K)])
         note("ag%d" % t, NENG, None, [], [ref("m%d" % t)])
 
     def col(j):
         return ref("col", j, j + 1)
-    PG, PL, PP, CF, THR, W1, W2, THA, THB, TH, BF8, BFX, BZ, C_WA, C_WB, THB0 = 0, 1, 2, 3, 4, 7, 8, 9, 10, 11, 12, 13, 14, 15, 16, 17
+    PG, PL, PP, CF, THR, W1, W2, THA, THB, TH, BF8, BFX, BZ, C_WA, C_WB, THB0, NTHR = 0, 1, 2, 3, 4, 7, 8, 9, 10, 11, 12, 13, 14, 15, 16, 17, 18
     B, Id = ref("B"), ref("Id")
     BIG = 8192.0
     iota(ref("pi"), [[1, 1]], 0, 1, False)
     iota(ref("cq"), [[1, 128]], 0, 0)
     iota(ref("cg"), [[1, 8], [0, 16]], 0, 0)
     iota(ref("cl", 0, 16), [[1, 16]], 0, 0)
-    fill(ref("CK"), 0.0)
     ts(ref("pj", 0, 1), ref("pi"), 4, A.arith_shift_right)
     ts(ref("pj", 1, 2), ref("pi"), 15, A.bitwise_and)
     fill(ref("C6"), 6144.0)
@@ -210,61 +228,73 @@ def rank_program(g, core, T, topo):
     fill(ref("Z"), 0.0)
     ts(Id, ref("cq"), col(PP), A.is_equal)
     ts(B, ref("cg"), col(PG), A.is_equal)
+    fill(ref("C7"), 191.0 * 1024)
     ts(ref("eq"), ref("cl", 0, 16), col(PL), A.is_equal)
-    fill(ref("O", 0, 16), 0.0)
-    ts(col(CF), col(PL), -64.0, A.mult, 0.5, A.add)
+    ts(col(CF), col(PL), -1.0, A.mult, 0.5, A.add)
     act(ref("NI4"), Id, AF.Copy, scale=-4096.0)
+    act(ref("NI7"), Id, AF.Copy, scale=-131072.0)
     tt(ref("BmI"), B, Id, A.subtract)
+    cp(ref("col", W1, W1 + 2), ref("wti"))
     ts(ref("cw"), ref("eq"), -17.0, A.mult, 1.0, A.add)
     cp(ref("B8"), ref("B", 0, 128, 16))
-    cp(ref("col", W1, W1 + 2), ref("wti"))
     ts(col(THB0), col(CF), -1.0, A.mult, 0.5, A.add)
-    ts(col(BF8), col(CF), BIG, A.mult)
-    ts(col(BFX), col(CF), 128.0, A.mult, -64.0, A.add)
     ts(ref("Wa"), ref("BmI"), col(W1), A.mult)
     ts(ref("Wb"), ref("BmI"), col(W2), A.mult)
-    for name, src, s in (("HI", "Id", 0.5), ("MI", "Id", -1.0), ("I8K", "Id", BIG), ("NHI", "Id", -0.5), ("I64", "Id", 64.0), ("NB", "B", -1.0),
-                         ("B8K", "B", BIG), ("NB8K", "B", -BIG), ("NB128", "B", -128.0)):
+    ts(ref("Wc"), ref("BmI"), col(W1), A.mult, 32.0, A.mult)
+    ts(col(BF8), col(CF), BIG, A.mult, -8.0, A.add)
+    ts(col(BFX), col(CF), 8 * BIG, A.mult, 64.0 - 8 * BIG, A.add)
+    fill(ref("CK"), 0.0)
+    for name, src, s in (("NB", "B", -1.0), ("W7", "B", -7 * BIG), ("NB8K", "B", -BIG), ("MI", "Id", -1.0), ("I8K", "Id", BIG)):
         act(ref(name), ref(src), AF.Copy, scale=s)
-    keep_where(ref("L"), B, [[1, 128]], A.is_gt, 0.0, -1)
-    keep_where(ref("G"), B, [[-1, 128]], A.is_gt, 0.0, 1)
+    keep_where(ref("L"), ref("NB"), [[1, 128]], A.is_gt, 0.0, -1)
+    keep_where(ref("WF"), ref("L"), [[1, 128]], A.not_equal, 0.5, -1)
+
+    def fallback(t):
+        keep_where(ref("Wv%d" % t), ref("WF"), [[0, 128]], A.is_equal, 0.0, 0)
+        keep_where(ref("G"), ref("WF", t, 128, 16), [[16, 8]], A.is_ge, -1.0 / 32, -1, t)
+        keep_where(ref("Wv%d" % t, t, 128, 16), ref("G"), [[16, 8]], A.is_ge, 0.0, -1, 15)
+    fallback(0)
+    keep_where(ref("NL8K"), ref("NB8K"), [[1, 128]], A.is_gt, 0.0, -1)
+    keep_where(ref("WL"), ref("W7"), [[1, 128]], A.not_equal, -8 * BIG, -1)
     iota(ref("i64"), [[1, 64]], 0, 0)
     iota(ref("ci"), [[16, 24]], -2048 - K, 0)
     iota(ref("sbi", p=64), [[0, 512]], 63, 1)
-    iota(ref("rs0"), [[0, K]], 0, 0)
-    iota(ref("mk0", p=16), [[0, K]], -8192, 0)
+    iota(ref("rs0"), [[0, CH]], 0, 0)
+    iota(ref("mk0", p=16), [[0, K]], 7 * 8192, 0)
     keep_where(ref("SEL", p=64), ref("sbi", p=64), [[-16, 4], [0, 8], [-1, 16]], A.is_equal, 0.0, 1)
-    keep_where(ref("rs"), ref("rs0"), [[0, 24], [1, 16]], A.not_equal, -2.0 ** 31, 0)
+    keep_where(ref("rs"), ref("rs0"), [[0, 8], [1, 16]], A.not_equal, -2.0 ** 31, 0)
     keep_where(ref("mk", p=16), ref("mk0", p=16), [[0, 24], [-1, 16]], A.is_equal, -2.0 ** 30, 1)
+    keep_where(ref("mj", p=16), ref("rs0", p=16), [[0, 8], [-1, 16]], A.is_equal, -2.0 ** 30, 1)
     keep_where(ref("EQ", p=16), ref("one", p=16), [[0, 8], [-1, 16]], A.is_equal, 0.0, 1)
+    fallback(1)
+    fallback(2)
 
-    def constants_v():
-        ts(ref("WF"), ref("L"), -64.0, A.mult)
-        ts(ref("G"), ref("G"), -1.0 / 32, A.mult)
+    def thresholds():
         ts(ref("pj", 2, 3), ref("thi"), 4, A.arith_shift_right)
         ts(ref("pj", 3, 4), ref("thi"), 15, A.bitwise_and)
         cp(col(TH), ref("thi"))
-        tt(ref("WF"), ref("WF"), ref("HI"), A.add)
         cp(ref("col", THA, THA + 2), ref("pj", 2, 4))
-        for t in range(VIS):
-            cp(ref("Wv%d" % t), ref("WF"))
-        for t in range(VIS):
-            tt(ref("Wv%d" % t, t, 128, 16), ref("WF", t, 128, 16), ref("G", t, 128, 16), A.add)
+        ts(col(BZ), col(TH), -0.5 - BIG, A.add)
+        ts(col(C_WA), col(THA), 16.0 / BIG ** 2, A.mult, -4096.0 / BIG ** 2, A.add)
+        ts(col(C_WB), col(THB), 1.0 / BIG ** 2, A.mult, -0.5 / BIG ** 2, A.add)
+        ts(ref("cim"), ref("ci"), col(PL), A.add)
+        ts(ref("WFA"), ref("B8"), col(C_WA), A.mult)
+        ts(ref("WFB"), ref("B8"), col(C_WB), A.mult)
+        for name, src, s in (("I64", "Id", 64.0), ("B8K", "B", BIG), ("NB128", "B", -128.0), ("B4K", "B", BIG / 2), ("NB4K", "B", -BIG / 2)):
+            ts(ref(name), ref(src), s, A.mult)
 
     def constants_s():
-        act(ref("Z", 15, 128, 16), ref("B8"), AF.Copy)
-        act(ref("WX"), ref("WF"), AF.Copy, scale=128.0)
-        act(ref("BmI8K"), ref("BmI"), AF.Copy, scale=BIG)
-        act(col(C_WA), col(THA), AF.Identity, scale=-16.0 / BIG, bias=4096.0 / BIG)
-        act(col(C_WB), col(THB), AF.Copy, scale=-1.0 / BIG)
-        act(col(BZ), col(TH), AF.Identity, scale=-BIG, bias=(1.0 - BIG) * BIG)
-        for name, j, s in (("PP", 0, 0.5), ("PP", 8, 0.5), ("PM", 0, 0.5), ("PM", 8, -0.5)):
-            act(ref(name, j, j + 8), ref("B8"), AF.Copy, scale=s)
         for t in range(VIS):
             act(col(THR + t), ref("eq", t, t + 1), AF.Identity, scale=-0.5 + (14 - t) / 32.0, bias=col(THB0))
-        act(ref("WFA"), ref("B8"), AF.Copy, scale=col(C_WA))
-        act(ref("WFB"), ref("B8"), AF.Copy, scale=col(C_WB))
-        act(ref("cim"), ref("ci"), AF.Identity, bias=col(PL))
+        act(ref("WX"), ref("WF"), AF.Copy, scale=8 * BIG)
+        for k in range(16):
+            act(ref("CK", 129 * k, 128 * k + 128, 16), ref("B8"), AF.Copy, scale=ref("cw", k, k + 1))
+        act(ref("col", NTHR, NTHR + VIS), ref("col", THR, THR + VIS), AF.Copy, scale=-1.0)
+
+    def narrow():
+        act(ref("Z", 15, 128, 16), ref("B8"), AF.Copy)
+        for name, j, s in (("PP", 0, 0.5), ("PP", 8, 0.5), ("PM", 0, 0.5), ("PM", 8, -0.5), ("WFC", 0, 1.5), ("WFD", 0, -1.0 / BIG)):
+            act(ref(name, j, j + 8), ref("B8"), AF.Copy, scale=s)
 
     def bk(b, lo=0, hi=K, p=128):
         return ref("b%d" % b, lo, hi, p=p)
@@ -272,63 +302,70 @@ def rank_program(g, core, T, topo):
     def blk(name, c):
         return ref(name, CH * c, CH * c + CH)
 
-    def wrap(out, src, lo, hi, first=True, last=True):
-        group(out, [(ref("Z", 15 - r, 143 - r), ref(src, lo + r, hi, 16)) for r in range(16)], first, last)
+    def wrap(out, src, lo, hi):
+        group(out, [(ref("Z", 15 - r, 143 - r), ref(src, lo + r, hi, 16)) for r in range(16)])
 
-    HS, HU = (5, 2, 7), (3, 1, 0)
+    HS, HU = (6, 2, 7), (3, 1, 5)
 
     def hash_sums(t, c):
-        xs = blk("x%d" % t, c)
-        mm(bk(HS[c], 0, CH), ref("Wa"), xs, True, True)
-        mm(bk(HS[c], CH, 2 * CH), ref("Wb"), xs, True, True)
-        group(bk(HU[c], 0, CH), [("C6", ref("one")), ("Wa", xs)], True, False)
-        act(ref("Mh", 2 * CH * c, 2 * CH * (c + 1)), bk(HS[c], 0, 2 * CH), AF.Identity, bias=192.0 - 4095.0 / 8192.0, scale=1.0 / 4096.0)
+        if t < VIS:
+            xs = blk("x%d" % t, c)
+            mm(bk(HS[c], 0, CH), ref("Wa"), xs, True, True)
+            mm(bk(HS[c], CH, 2 * CH), ref("Wb"), xs, True, True)
+
+    def hash_floors(t, c):
+        if t < VIS:
+            act(ref("Mh", 2 * CH * c, 2 * CH * (c + 1)), bk(HS[c], 0, 2 * CH), AF.Identity, bias=192.0 - 4095.0 / 8192.0, scale=1.0 / 4096.0)
 
     def hash_rests(t, c):
-        e = 2 * CH * c
-        group(bk(HS[c], 2 * CH, 3 * CH), [("Wb", blk("x%d" % t, c)), ("NI4", ref("Mh", e + CH, e + 2 * CH))])
-        mm(bk(HU[c], 0, CH), ref("NI4"), ref("Mh", e, e + CH), False, True)
-        act(blk("UP", c), bk(HS[c], 2 * CH, 3 * CH), AF.Identity, bias=786432.0)
+        if t < VIS:
+            e, xs = 2 * CH * c, blk("x%d" % t, c)
+            group(bk(HS[c], 2 * CH, 3 * CH), [("Wb", xs), ("NI4", ref("Mh", e + CH, e + 2 * CH))])
+            group(bk(HU[c], 0, CH), [("C6", ref("one")), ("Wa", xs), ("NI4", ref("Mh", e, e + CH))])
+
+    def hash_more(t, c):
+        if t < VIS:
+            group(bk(HU[c], CH, 2 * CH), [("C7", ref("one")), ("Wc", blk("x%d" % t, c)), ("NI7", ref("Mh", 2 * CH * c, 2 * CH * c + CH))])
+
+    def hash_other(t, c):
+        if t < VIS:
+            act(blk("UP", c), bk(HS[c], 2 * CH, 3 * CH), AF.Identity, bias=786432.0)
 
     def hash_step(c, j):
-        u = bk(HU[c], 0, CH)
         if j == 0:
-            tt(blk("pr", c), blk("UP", c), u, A.mult)
+            tt(blk("pr", c), blk("UP", c), bk(HU[c], 0, CH), A.mult)
         elif j == 1:
-            ts(blk("ps", c), blk("pr", c), 5, A.arith_shift_right)
+            tt(blk("pt", c), blk("pr", c), bk(HU[c], CH, 2 * CH), A.add)
         elif j == 2:
-            tt(blk("pt", c), blk("ps", c), u, A.add)
-        elif j == 3:
-            ts(blk("hi", c), blk("pt", c), 4095, A.bitwise_and)
+            ts(blk("hi", c), blk("pt", c), 5, A.arith_shift_right, 4095, A.bitwise_and)
         else:
             cp(blk("hu", c), blk("hi", c))
 
-    def spread(t, on_v, ks):
-        for k in ks:
+    def hash_next(t, c, j):
+        if t + 1 < VIS:
+            hash_step(c, j)
+
+    def spread(t, q, ks):
+        for k in ks if t < VIS else ():
             o, s = ref("X16", k, 16 * CH, 16), blk("x%d" % t, 0)
-            if on_v:
+            if q == "v":
                 cp(o, s)
+            elif q == "g":
+                keep_where(o, s, [[0, CH]], A.is_equal, 0.0, 0)
             else:
                 act(o, s, AF.Copy)
 
-    def hash_front(t):
-        def between(j):
-            spread(t, t == 0, (range(0, 4), range(4, 10), range(10, 16))[j])
-            if t == 0:
-                for k in (range(0, 6), range(6, 12), range(12, 16))[j]:
-                    act(ref("CK", 129 * k, 128 * k + 128, 16), ref("B8"), AF.Copy, scale=ref("cw", k, k + 1))
-        for c in (1, 0):
-            hash_sums(t, c)
-        between(0)
-        for c in (1, 0):
-            hash_rests(t, c)
-        hash_sums(t, 2)
-        between(1)
-        hash_rests(t, 2)
-        between(2)
+    XBK, HFB, TAB, FREE = 4, 5, 4, (1, 5, 7)
+    PART = ((0, 2 * CH), (2 * CH, K))
+    AT = ({"count": (0, 0), "lowest": (1, 0), "place": (1, 256), "letter": (2, 0), "pair": (0, 0), "kept": (2, 0), "half": (0, 256), "far": (3, 0)},
+          {"count": (6, 0), "lowest": (7, 0), "place": (7, 128), "letter": (6, 256), "pair": (6, 128), "kept": (6, 256), "half": (6, 384), "far": (6, 0)})
 
-    SB, VB, XBK, HFB, TAB = (0, 2, 6), (1, 3, 7), 4, 5, 7
-    PIECES = (0, 26, 52, 78, 104, 128)
+    def at(p, what, n=None, skip=0):
+        b, c = AT[p][what]
+        return bk(b, c + skip, c + skip + (PART[p][1] - PART[p][0] if n is None else n))
+
+    def part(name, p, per=1):
+        return ref(name, PART[p][0] // per, PART[p][1] // per)
 
     def look_v(i0, i1):
         tt(ref("D", 16 * i0, 16 * i1), ind(lexw, ref("hu", i0, i1)), ref("X16", 16 * i0, 16 * i1), A.not_equal)
@@ -341,36 +378,43 @@ def rank_program(g, core, T, topo):
             tt(ref("D", 16 * i0 + k, 16 * i1, 16), ref("C", 16 * i0 + k, 16 * i1, 16), bk(XBK, i0, i1), A.not_equal)
 
     def count(i0, i1):
-        c = i0 // CH
-        group(bk(SB[c], i0 - CH * c, i1 - CH * c), [(ref("CK", 128 * k, 128 * k + 128), ref("D", 16 * i0 + k, 16 * i1, 16)) for k in range(16)])
+        p = i0 // (2 * CH)
+        group(at(p, "count", i1 - i0, i0 - PART[p][0]), [(ref("CK", 128 * k, 128 * k + 128), ref("D", 16 * i0 + k, 16 * i1, 16)) for k in range(16)])
 
-    def pairs(c):
-        act(blk("pm", c), bk(SB[c], 0, CH), AF.Sign, bias=-13.5, scale=-1.0)
+    def pairs(p):
+        act(part("pm", p), at(p, "count"), AF.Sign, bias=-13.5, scale=-1.0)
 
-    def lowest(t, c):
-        pm = blk("pm", c)
-        mm(bk(VB[c], 0, CH), ref("Wv%d" % t), pm, True, True)
-        group(bk(SB[c], 2 * CH, 3 * CH), [("Id", blk("x%d" % t, c)), ("WX", pm)])
-        mm(bk(SB[c], CH, 2 * CH), ref("WF"), pm, True, True)
+    def lowest(t, p):
+        pm = part("pm", p)
+        group(at(p, "lowest"), [("Wv%d" % t, pm)])
+        group(at(p, "letter"), [("Id", part("x%d" % t, p)), ("WX", pm)])
 
-    def pair_lane(c):
-        act(blk("Fx", c), bk(SB[c], 2 * CH, 3 * CH), AF.Relu, bias=col(BFX))
-        act(blk("Fm", c), bk(SB[c], CH, 2 * CH), AF.Relu, bias=col(BF8), scale=BIG)
+    def pair_letter(p):
+        act(part("Fx", p), at(p, "letter"), AF.Relu, bias=col(BFX))
+
+    def pair_lane(p):
+        act(part("Fm", p), at(p, "letter"), AF.Relu, bias=col(BF8), scale=0.125)
 
     def lane(t, c):
-        ts(blk("Le", c), bk(VB[c], 0, CH), col(THR + t), A.is_ge)
+        ts(blk("Le", c), at(c // 2, "lowest", CH, CH * (c % 2)), col(THR + t), A.is_ge)
+
+    def lane_s(t, half):
+        if half == 0:
+            act(part("RF", 0), at(0, "lowest"), AF.Sign, bias=col(NTHR + t))
+        else:
+            act(part("Le", 0), part("RF", 0), AF.Relu)
 
     def place(c):
         tt(blk("Lh", c), blk("Le", c), bk(HFB, CH * c, CH * c + CH), A.mult)
 
-    def place_wrap(c):
-        wrap(bk(VB[c], CH, CH + 8), "Lh", CH * c, CH * c + CH)
+    def place_wrap(p):
+        wrap(at(p, "place", (PART[p][1] - PART[p][0]) // 16), "Lh", *PART[p])
 
-    def place_list(c):
-        ts(ref("le", 8 * c, 8 * c + 8), bk(VB[c], CH, CH + 8), 2048.0, A.add)
+    def place_list(p):
+        ts(part("le", p, 16), at(p, "place", (PART[p][1] - PART[p][0]) // 16), 2048.0, A.add)
 
-    def letters(c):
-        tt(blk("LC", c), ind(lexw, ref("le", 8 * c, 8 * c + 8)), blk("Le", c), A.mult)
+    def letters(p):
+        tt(part("LC", p), ind(lexw, part("le", p, 16)), part("Le", p), A.mult)
 
     def meanings(t, c):
         tt(blk("d", c), ind(mngw, ref("le", 8 * c, 8 * c + 8)), blk("m%d" % t, c), A.subtract)
@@ -378,14 +422,24 @@ def rank_program(g, core, T, topo):
     def distance(c):
         act(blk("ad", c), blk("d", c), AF.Abs)
 
-    def by_words_t(c):
-        group(bk(SB[c], 392, 408), [(blk("Fx", c), ref("PP")), (blk("LC", c), ref("PM"))])
-        group(bk(SB[c], 384, 392), [(blk("Fm", c), ref("WFA")), (blk("Fm", c), ref("WFB")), (blk("ad", c), ref("B8"))])
-        group(bk(SB[c], 0, CH), [("Id", blk("Fm", c)), ("B", blk("ad", c))])
+    def blocks(p):
+        return range(PART[p][0] // CH, PART[p][1] // CH)
 
-    def by_words_s(c):
-        act(ref("mr", 16 * c, 16 * c + 16), bk(SB[c], 392, 408), AF.Abs, bias=-32.0)
-        act(ref("nf", 8 * c, 8 * c + 8), bk(SB[c], 384, 392), AF.Relu, bias=-4095.0)
+    def halves_t(p):
+        for j, c in enumerate(blocks(p)):
+            group(at(p, "half", 16, 16 * j), [(blk("Fx", c), ref("PP")), (blk("LC", c), ref("PM"))])
+
+    def halves_s(p):
+        act(part("mr", p, 8), at(p, "half", 16 * len(blocks(p))), AF.Abs, bias=-32.0)
+
+    def free_t(c):
+        group(bk(FREE[c], 384, 392), [(blk("Le", c), ref("WFC")), (blk("Fm", c), ref("WFA")), (blk("Fm", c), ref("WFB")), (blk("ad", c), ref("WFD"))])
+
+    def far_t(p):
+        group(at(p, "far"), [("Id", part("Fm", p)), ("NB", part("ad", p))])
+
+    def free_pair(p):
+        act(part("Zf", p), at(p, "far"), AF.Sign, bias=col(BZ))
 
     def rows_s(c):
         for j in range(8):
@@ -396,7 +450,7 @@ def rank_program(g, core, T, topo):
         for j in range(8):
             q = 8 * c + j
             u = ref("U", 64 * q, 64 * q + 64)
-            ts(u, ref("ab", 64 * q, 64 * q + 64), ref("mr", 16 * c + 8 + j, 16 * c + 9 + j), A.is_equal, ref("nf", q, q + 1), A.mult)
+            ts(u, ref("ab", 64 * q, 64 * q + 64), ref("mr", 16 * c + 8 + j, 16 * c + 9 + j), A.is_equal, bk(FREE[c], 384 + j, 385 + j), A.is_gt)
 
     def rows_t(c):
         for j in range(8):
@@ -404,199 +458,144 @@ def rank_program(g, core, T, topo):
             u = ref("U", 64 * q, 64 * q + 64)
             mm(bk(TAB, 0, 64, p=64), u, u, q == 0, q == 23)
 
-    def side_t(t, c):
-        group(bk(SB[c], CH, 2 * CH), [("B", blk("Fx", c))])
-        group(bk(SB[c], 2 * CH, 3 * CH), [("Id", blk("x%d" % t, c)), ("I8K", blk("Le", c)), ("MI", blk("Fm", c))])
+    def pair_t(p):
+        group(at(p, "pair"), [("B", part("Fx", p))])
 
-    def side_s(c):
-        act(blk("Xf", c), bk(SB[c], CH, 2 * CH), AF.Identity, bias=-1.0)
-        act(blk("xp", c), bk(SB[c], 2 * CH, 3 * CH), AF.Copy)
+    def pair_s(p):
+        act(part("Xf", p), at(p, "pair"), AF.Identity, bias=-1.0)
 
-    def not_free(c):
-        act(blk("Zf", c), bk(SB[c], 0, CH), AF.Relu, bias=col(BZ), scale=BIG)
+    def kept_t(t, p):
+        group(at(p, "kept"), [("Id", part("x%d" % t, p)), ("I8K", part("Le", p)), ("MI", part("Fm", p))])
 
-    WB, Z1, MB, DB, S1, GB, Z2 = 4, 5, 2, 3, 1, 7, (0, 6, 4)
+    def kept_s(p):
+        act(part("xp", p), at(p, "kept"), AF.Copy)
 
-    def same_place(c):
-        mm(bk(Z2[c], 0, CH), ref("NB8K"), blk("O", c), False, False)
+    WB, Z1, MB, HB, DB, GB, ZB = (0, 6), 5, 2, 3, 7, 4, (0, 3, 1)
+    pw, lfw, again = bk(2, 256, 304), bk(1, 272, 296), bk(2, 384, 512)
+
+    def table_rows():
+        for b in range(4):
+            mm(bk(TAB, 64 + 64 * b, 128 + 64 * b), ref("SEL", 128 * b, 128 * b + 128, p=64), ref("TS", p=64), True, True)
+
+    def found_t(p):
+        group(bk(WB[p], *PART[p]), [("Id", part("LC", p)), ("WL", part("Le", p)), ("B", part("Fm", p))], True, False)
+
+    def flagged(p):
+        tt(part("RF", p), ind(ref("TW"), part("lf", p, 16)), part("Xf", p), A.is_equal)
+
+    def new_letters(xn, p):
+        tt(part(xn, p), part("xp", p), bk(WB[p], *PART[p]), A.min)
+
+    def zb(c, lo=0, hi=CH):
+        return bk(ZB[c], lo, hi)
+
+    def ends(name, c):
+        return ref(name, CH * c + 15, CH * c + CH, 16)
+
+    def listed(name, c):
+        return ref(name, 8 * c, 8 * c + 8)
+
+    def row(q, lo, hi):
+        return ("E", CH * q + lo, CH * q + hi, T["E"][:, q, lo:hi], 1)
+
+    def same_v(c):
+        for q in range(8 * c, 8 * c + 8):
+            i0, i1 = 16 * q, CH * (c + 1)
+            ts(row(q, 0, i1 - i0), ref("Hb", i0, i1), ref("s1", i0 + 15, i0 + 16), A.is_equal)
+
+    def same_s(half):
+        for q in range(8):
+            apart = ref("ab", CH * q, CH * q + CH - 16 * q)
+            if half == 0:
+                act(apart, bk(2, 384 + 16 * q, 512), AF.Abs, bias=ref("s1", 16 * q + 15, 16 * q + 16), scale=-1.0)
+            else:
+                act(row(q, 0, CH - 16 * q), apart, AF.Relu, bias=1.0, scale=-1.0)
+
+    def same_t(c):
         for j in range(7):
-            q = 8 * c + j
-            i0, i1 = 16 * q + 16, CH * (c + 1)
-            e = ref("E", CH * q, CH * q + i1 - i0)
-            ts(e, ref("Hb", i0, i1), bk(S1, 16 * q + 15, 16 * q + 16), A.is_equal)
-            mm(bk(Z2[c], i0 - CH * c, CH), ref("NB8K"), e, False, j == 6)
-
-    def writers(c):
-        scan(blk("sj", c), ref("rs", 0, CH), bk(Z2[c], 0, CH), A.add, A.max)
-
-    def writers_places(c):
-        tt(ref("z", 8 * c, 8 * c + 8), ref("sj", CH * c + 15, CH * c + CH, 16), ref("cim", 8 * c, 8 * c + 8), A.max)
-
-    def writers_list(c):
-        ts(ref("lo", 8 * c, 8 * c + 8), ref("z", 8 * c, 8 * c + 8), 2048.0 + K, A.add)
+            mm(zb(c, 16 * j + 16), ref("NB8K"), row(8 * c + j, 16, CH - 16 * j), False, False)
+        mm(zb(c), ref("NL8K"), ("E", 8 * CH * c, 8 * CH * (c + 1), T["E"][:, 8 * c:8 * c + 8, 0:16], 1), False, True)
 
     def scatter(buf, src, c):
-        w, o, s = ref(buf), ref("lo", 8 * c, 8 * c + 8), blk(src, c)
+        w, o, s = ref(buf), listed("lo", c), blk(src, c)
         do("v", lambda: g.vector.tensor_copy(w[3].indirect(o[3]), s[3]), [o, s], [w])
 
-    hash_front(0)
-    constants_v()
+    spread(0, "v", range(16))
+    for c in (1, 0, 2):
+        hash_sums(0, c)
+        hash_floors(0, c)
+    for c in (1, 0, 2):
+        hash_rests(0, c)
+        hash_more(0, c)
+        hash_other(0, c)
     constants_s()
-    for j in range(5):
+    for j in range(4):
         for c in (1, 0):
             hash_step(c, j)
     for t in range(VIS):
-        x, m, last = "x%d" % t, "m%d" % t, t == VIS - 1
+        x, m, last, u = "x%d" % t, "m%d" % t, t == VIS - 1, t + 1
         xn, gn = "xn%d" % t, "gn%d" % t
         to = (rank + 2) % N if last else (rank - 1) % N
 
-        def old_meanings(c):
-            if t > 0:
-                scatter("mn", "gn%d" % (t - 1), c)
+        step = {
+            "hash": hash_step, "look_v": look_v, "look_s": look_s, "compare": compare, "count": count,
+            "words_t": lambda: mm(bk(XBK, CH, K), Id, ref(x, CH, K), True, True),
+            "places_v": lambda: ts(ref("hf"), ref("hu"), -2048.0, A.add),
+            "places_t": lambda: mm(bk(HFB), Id, ref("hf"), True, True),
+            "pairs": pairs, "lowest": lambda p: lowest(t, p), "pair_letter": pair_letter, "pair_lane": pair_lane,
+            "lane": lambda c: lane(t, c), "lane_s": lambda h: lane_s(t, h), "narrow": lambda: t == 0 and narrow(),
+            "place": place, "place_wrap": place_wrap, "place_list": place_list,
+            "old_meanings": lambda c: scatter("mn", "gn%d" % (t - 1), c) if t > 0 else (c == 0 and thresholds()),
+            "letters": letters, "pair_t": pair_t, "pair_s": pair_s, "kept_t": lambda p: kept_t(t, p), "kept_s": kept_s,
+            "meanings": lambda c: meanings(t, c), "distance": distance, "free_t": free_t, "far_t": far_t, "not_free": free_pair,
+            "halves_t": halves_t, "halves_s": halves_s, "rows_s": rows_s, "rows_v": rows_v, "rows_t": rows_t,
+            "table": lambda: ts(ref("TS", p=64), bk(TAB, 0, 64, p=64), 1.0, A.min), "table_t": table_rows,
+            "table_v": lambda: cp(ref("TW"), bk(TAB, 64, 320)), "code_wrap": lambda: wrap(pw, "FL", 0, 2 * K),
+            "own_high": lambda: act(ref("XB"), bk(2, 256, 280), AF.Identity, bias=128.0 - 15.0 / 32, scale=1.0 / 16),
+            "code_low": lambda: act(ref("CB"), bk(2, 280, 304), AF.Copy), "code_high": lambda: group(lfw, [("Id", ref("CB")), ("I64", ref("XB"))]),
+            "code_list": lambda: ts(ref("lf"), lfw, -64.0 * 132, A.add), "flagged": flagged,
+            "found_t": found_t, "found_far": lambda p: mm(bk(WB[p], *PART[p]), ref("NB4K"), part("Zf", p), False, False),
+            "found_flag": lambda p: mm(bk(WB[p], *PART[p]), ref("B8K"), part("RF", p), False, True),
+            "new_letters": lambda p: new_letters(xn, p), "send_letters": lambda p: send(part(xn, p), part("x%d" % u, p), to, "%sx%d" % ("ab"[p], u)),
+            "merge_t": lambda j: mm(bk(MB), ref(("B4K", "NB8K")[j - 1]), ref(("Zf", "RF")[j - 1]), j == 1, j == 2),
+            "merge": lambda: act(ref("M"), bk(MB), AF.Relu, scale=1.0 / BIG, bias=8.0),
+            "half": lambda: act(ref("ha"), ref("ad"), AF.Identity, bias=127.8, scale=0.5),
+            "below": lambda: act(ref("nd"), ref("d"), AF.Relu, scale=-1.0),
+            "mean_t": lambda: group(bk(DB), [("NB128", ref("Le")), ("MI", ref("nd"))], True, False),
+            "mean_half": lambda: mm(bk(DB), Id, ref("ha"), False, True), "mean_v": lambda: tt(ref("gd"), ref("M"), bk(DB), A.mult),
+            "new_t": lambda j: mm(bk(GB), Id, ref((m, "gd")[j]), j == 0, j == 1), "new_meanings": lambda: act(ref(gn), bk(GB), AF.Copy),
+            "send_meanings": lambda: send(ref(gn), ref("m%d" % u), to, "ag%d" % u),
+            "all_t": lambda: mm(bk(HB, CH, K), B, ref("Lh", CH, K), True, True), "all_v": lambda c: cp(blk("Hb", c), bk(HB, CH * c, CH * c + CH)),
+            "again_t": lambda: mm(again, B, blk("Lh", 0), True, True),
+            "masked_t": lambda: group(bk(Z1), [(ref("EQ", p=16), ref("mk", p=16)), ("B", ref("Lh"))], True, False),
+            "merging_t": lambda j: mm(bk(Z1), ref(("B4K", "NB8K")[j - 1]), ref(("Zf", "RF")[j - 1]), False, j == 2),
+            "mergers": lambda c: scan(blk("s1", c), ref("rs"), bk(Z1, CH * c, CH * c + CH), A.add, A.max),
+            "places_again": lambda c: mm(zb(c), ref("EQ", p=16), ref("mj", p=16), True, False),
+            "same_v": same_v, "same_s": same_s, "same_t": same_t,
+            "writers": lambda c: scan(blk("sj", c), ref("rs"), zb(c), A.add, A.max),
+            "merged_again": lambda c: tt(listed("zz", c), ends("sj", c), ends("s1", c), A.add),
+            "writers_places": lambda c: tt(listed("z", c), listed("zz", c), listed("cim", c), A.max),
+            "writers_list": lambda c: ts(listed("lo", c), listed("z", c), 2048.0 + K, A.add), "write": lambda c: scatter("lx", xn, c),
+            "sum_before": lambda j: last and act(ref("C", 1024 * j, 1024 * j + 1024), ref("mn", K + 1024 * j, K + 1024 * j + 1024), AF.Copy,
+                                                 accum=ref("ya", j, j + 1)),
+            "keep": lambda: last and act(ref("mn", 0, K), bk(GB), AF.Copy),
+            "change": lambda c: last and tt(blk("df", c), ind(ref("mn"), listed("lo", c)), blk(gn, c), A.subtract),
+            "write_meanings": lambda c: (last or c == 2) and scatter("mn", gn, c),
+            "changes": lambda: last and act(ref("D", 0, 2 * CH), ref("df", CH, K), AF.Copy, scale=-1.0, accum=ref("ya", 4, 5)),
+            "sums_v": lambda: last and do("v", lambda: g.vector.tensor_reduce(ref("yb")[3], ref("ya")[3], AxisListType.X, A.add), [ref("ya")], [ref("yb")]),
+            "sums": lambda c: hash_sums(u, c), "floors": lambda c: hash_floors(u, c), "rests": lambda c: hash_rests(u, c), "other": lambda c: hash_other(u, c),
+            "more": lambda c: hash_more(u, c),
+            "next": lambda c, j: hash_next(t, c, j), "spread_s": lambda a, b: spread(u, "s", range(a, b)), "spread_g": lambda a, b: spread(u, "g", range(a, b)),
+        }
+        for call in ORDER.replace("\n", " ").split(","):
+            name, *args = call.split()
+            step[name](*[int(a) for a in args])
 
-        look_s(128, 192)
-        look_s(192, 256)
-        mm(bk(XBK), Id, ref(x), True, True)
-        for j in range(5):
-            hash_step(2, j)
-            look_v(PIECES[j], PIECES[j + 1])
-        look_s(256, 320)
-        look_s(320, 384)
-        ts(ref("hf"), ref("hu"), -2048.0, A.add)
-        count(0, 128)
-        mm(bk(HFB), Id, ref("hf"), True, True)
-        for i in (128, 192, 256):
-            compare(i, i + 64)
-            count(i, i + 64)
-        for c in (0, 1):
-            pairs(c)
-        for c in (0, 1):
-            lowest(t, c)
-        compare(320, 384)
-        count(320, 384)
-
-        for c in (0, 1):
-            pair_lane(c)
-        for c in (0, 1):
-            lane(t, c)
-        for c in (0, 1):
-            place(c)
-        pairs(2)
-        place_wrap(0)
-        lowest(t, 2)
-        place_wrap(1)
-        old_meanings(2)
-        place_list(0)
-        old_meanings(1)
-        lane(t, 2)
-        pair_lane(2)
-        old_meanings(0)
-        place(2)
-        for c in (0, 1):
-            side_t(t, c)
-        place_wrap(2)
-        meanings(t, 0)
-        place_list(1)
-        letters(0)
-        side_s(0)
-        side_s(1)
-        distance(0)
-        meanings(t, 1)
-        by_words_t(0)
-        place_list(2)
-        letters(1)
-        distance(1)
-        by_words_s(0)
-        meanings(t, 2)
-        letters(2)
-        by_words_t(1)
-        side_t(t, 2)
-        pw, lfw = bk(VB[1], 2 * CH, 2 * CH + 24), bk(VB[0], 2 * CH, 2 * CH + 24)
-        wrap(pw, "Fx", 0, K)
-        rows_s(0)
-        distance(2)
-        by_words_t(2)
-        by_words_s(1)
-        rows_v(0)
-        rows_s(1)
-        by_words_s(2)
-        rows_t(0)
-        wrap(lfw, "LC", 0, K, True, False)
-        rows_v(1)
-        rows_s(2)
-        act(ref("XB"), pw, AF.Identity, bias=128.0 - 15.0 / 32, scale=1.0 / 16)
-        rows_t(1)
-        rows_v(2)
-        rows_t(2)
-        mm(lfw, ref("I64"), ref("XB"), False, True)
-        mm(bk(DB), B, ref("Lh"), True, True)
-        side_s(2)
-        for c in range(3):
-            not_free(c)
-        act(ref("ha"), ref("ad"), AF.Identity, bias=127.8, scale=0.5)
-
-        ts(ref("TS", p=64), bk(TAB, 0, 64, p=64), 1.0, A.min)
-        ts(ref("lf"), lfw, -64.0 * 132, A.add)
-        for b in range(4):
-            mm(bk(TAB, 64 + 64 * b, 128 + 64 * b), ref("SEL", 128 * b, 128 * b + 128, p=64), ref("TS", p=64), True, True)
-        cp(ref("Hb"), bk(DB))
-        cp(ref("TW"), bk(TAB, 64, 320))
-        group(bk(WB), [("Id", ref("LC")), ("BmI8K", ref("Le")), ("B", ref("Zf"))], True, False)
-        group(bk(Z1), [(ref("EQ", p=16), ref("mk", p=16)), ("B", ref("Lh")), ("B", ref("Fm")), ("NB", ref("Zf"))], True, False)
-        group(bk(MB), [("B", ref("Fm")), ("NB", ref("Zf"))], True, False)
-        tt(ref("RF"), ind(ref("TW"), ref("lf")), ref("Xf"), A.is_equal)
-        mm(bk(WB), ref("B8K"), ref("RF"), False, True)
-        mm(bk(Z1), ref("NB8K"), ref("RF"), False, True)
-        mm(bk(MB), ref("NB8K"), ref("RF"), False, True)
-        group(bk(DB), [("HI", ref("d")), ("NHI", ref("ad")), ("Id", ref("ha")), ("NB128", ref("Le"))])
-
-        tt(ref(xn), ref("xp"), bk(WB), A.min)
-        send(ref(xn), ref("x%d" % (t + 1)), to, "ax%d" % (t + 1))
-        act(ref("M"), bk(MB), AF.Relu, scale=1.0 / BIG)
-        scan(bk(S1), ref("rs"), bk(Z1), A.add, A.max)
-        mm(bk(GB), Id, ref(m), True, False)
-        for c in (2, 1, 0):
-            group(bk(Z2[c], 0, CH), [(ref("EQ", p=16), ref("mk", 0, CH, p=16)), ("B", blk("Lh", c)), ("I8K", blk("M", c))], True, False)
-        tt(ref("O", 1, K), ref("Hb", 1, K), bk(S1, 0, K - 1), A.is_equal)
-        tt(ref("gd"), ref("M"), bk(DB), A.mult)
-        mm(bk(GB), Id, ref("gd"), False, True)
-        act(ref(gn), bk(GB), AF.Copy)
-        send(ref(gn), ref("m%d" % (t + 1)), to, "ag%d" % (t + 1))
-        same_place(2)
-        same_place(1)
-        writers(2)
-        same_place(0)
-        writers_places(2)
-        writers(1)
-        writers_list(2)
-        writers_places(1)
-        writers(0)
-        if not last:
-            hash_front(t + 1)
-        scatter("lx", xn, 2)
-        writers_list(1)
-        writers_places(0)
-        scatter("lx", xn, 1)
-        writers_list(0)
-        if last:
-            scatter("mn", gn, 2)
-            scatter("lx", xn, 0)
-            store("y", T.yx[:, :], ref("x3"), "ox")
-            store("y", T.yl[:, :], lexw, "ol")
-            store("y", T.yg[:, :], ref("m3"), "og")
-            scatter("mn", gn, 1)
-            scatter("mn", gn, 0)
-        else:
-            for j in range(5):
-                for c in (1, 0):
-                    hash_step(c, j)
-                if j == 0:
-                    scatter("lx", xn, 0)
-
-    act(ref("D", 0, W - 2 * SUMV), ref("mn", K + 2 * SUMV, K + W), AF.Copy, accum=ref("ya"))
-    scan(ref("run"), ref("mn", K, K + SUMV), ref("mn", K + SUMV, K + 2 * SUMV), A.add, A.add)
-    tt(ref("yb"), ref("ya"), ref("run", SUMV - 1, SUMV), A.add)
-    store("y", T.ym[:, :], ref("yb"), "om")
+    store("y", T.yl[:, :], lexw, "ol")
+    store("y", T.yx[:, :], ref("x3"), "ox")
+    store("y", T.yg[:, :], ref("m3"), "og")
+    scan(blk("sj", 0), ref("one"), blk("df", 0), A.mult, A.subtract, ref("yb"))
+    store("s", T.ym[:, :], ref("sj", CH - 1, CH), "om")
     for q in ("v", "s", "t", "g"):
         g.wait_ge(T.sem[own[q]], cnt[q])
     g.wait_ge(T.sem["rl"], sent[0])

from concourse.mybir import dt, AluOpType, AxisListType, ActivationFunctionType

N, W, K, VIS = 6, 4096, 384, 3
CH = 128
NENG = 8
BF, F32, I32, U16, F16 = "bfloat16", "float32", "int32", "uint16", "float16"
SCRATCH = {
    "lx": ("sbuf", [128, K + W], BF), "mn": ("sbuf", [128, K + W], BF),
    "wti": ("sbuf", [128, 2], I32), "thi": ("sbuf", [128, 1], I32), "pi": ("sbuf", [128, 1], I32), "pj": ("sbuf", [128, 4], I32),
    "col": ("sbuf", [128, 24], F32), "i64": ("sbuf", [128, 64], BF), "one": ("sbuf", [128, 128], BF),
    "X16": ("sbuf", [128, 16 * CH], BF), "C": ("sbuf", [128, 16 * K], BF), "D": ("sbuf", [128, 16 * K], BF), "E": ("sbuf", [128, 24, CH], BF),
    "UP": ("sbuf", [128, K], F32), "Mh": ("sbuf", [128, 2 * K], BF),
    "hu": ("sbuf", [128, K], U16), "hf": ("sbuf", [128, K], F16), "Lh": ("sbuf", [128, K], F16), "Hb": ("sbuf", [128, K], F16),
    "le": ("sbuf", [128, 24], U16), "lf": ("sbuf", [128, 24], U16), "lo": ("sbuf", [128, 24], U16),
    "ab": ("sbuf", [128, 1536], BF), "U": ("sbuf", [128, 1536], BF), "TS": ("sbuf", [128, 64], BF), "TW": ("sbuf", [128, 256], BF),
    "ya": ("sbuf", [128, 5], F32), "yb": ("sbuf", [128, 1], F32), "CK": ("sbuf", [128, 2048], BF), "Z": ("sbuf", [128, 144], BF),
    "mr": ("sbuf", [128, 48], F32), "XB": ("sbuf", [128, 24], BF), "CB": ("sbuf", [128, 24], BF), "FL": ("sbuf", [128, 2 * K], BF),
    "PP": ("sbuf", [128, 16], BF), "PM": ("sbuf", [128, 16], BF), "sj": ("sbuf", [128, K], F32), "s1": ("sbuf", [128, K], F32),
}
for _n in ("x0 x1 x2 x3 m0 m1 m2 m3 xn0 xn1 xn2 gn0 gn1 gn2 pm Le Fm d ad nd ha Zf Xf xp RF M gd df mk mk0").split():
    SCRATCH[_n] = ("sbuf", [128, K], BF)
for _n in ("cg cl cq B Id BmI L WF WX Wv0 Wv1 Wv2 Wa Wb Wc C6 C7 NI4 NI7 MI NB B8K NB8K NL8K I8K WL W7 B4K NB4K NB128 I64 EQ rs rs0 mj").split():
    SCRATCH[_n] = ("sbuf", [128, 128], BF)
for _n in ("B8 G WFA WFB WFC WFD").split():
    SCRATCH[_n] = ("sbuf", [128, 8], BF)
for _n in ("sbi SEL").split():
    SCRATCH[_n] = ("sbuf", [128, 512], BF)
for _n in ("pr pt hi").split():
    SCRATCH[_n] = ("sbuf", [128, K], I32)
for _n in ("eq cw").split():
    SCRATCH[_n] = ("sbuf", [128, 16], F32)
for _n in ("ci cim z zz").split():
    SCRATCH[_n] = ("sbuf", [128, 24], F32)
for _b in range(8):
    SCRATCH["b%d" % _b] = ("psum", [128, 512], F32)
SIDE = {"Fx": 0, "LC": K}
SEMAPHORES = ["qv", "qs", "qt", "qg", "lx", "lw", "lt", "lg", "ll", "lm", "ax1", "bx1", "ag1", "ax2", "bx2", "ag2", "ax3", "bx3", "ag3",
              "rl", "ox", "og", "ol", "om"]
ORDER = """look_s 128 192, look_s 192 256, look_v 0 24, hash 2 0, look_v 24 44, hash 2 1, look_v 44 64, hash 2 2, look_v 64 84, hash 2 3, look_s 256 320,
look_v 84 128, places_v, words_t, count 0 64, compare 128 192, count 128 192, compare 192 256, count 64 128, places_t, count 192 256, look_s 320 384,
compare 256 320, count 256 320, compare 320 384, pairs 0, lowest 0, narrow, lane_s 0, lane_s 1, count 320 384, pairs 1, pair_letter 0, pair_lane 0,
lowest 1, pair_letter 1, pair_lane 1, old_meanings 1, place 0, place 1, place_wrap 0, pair_t 0, kept_t 0, pair_s 0, kept_s 0, old_meanings 0, lane 2,
kept_t 1, place_list 0, place 2, letters 0, meanings 0, place_wrap 1, halves_t 0, meanings 1, distance 0, pair_t 1, free_t 0, place_list 1, letters 1,
meanings 2, halves_s 0, distance 1, free_t 1, halves_t 1, rows_s 0, rows_v 0, rows_s 1, rows_v 1, code_wrap, far_t 0, halves_s 1, distance 2,
free_t 2, rows_t 0, rows_t 1, rows_s 2, own_high, kept_s 1, code_low, rows_v 2, rows_t 2, table, code_high, code_list, far_t 1, not_free 0, all_t,
all_v 2, all_v 1, found_t 1, table_t, table_v, half, sum_before 0, not_free 1, pair_s 1, below, sum_before 1, flagged 0, again_t, found_t 0,
found_far 0, masked_t, merging_t 1, found_far 1, flagged 1, found_flag 0, merge_t 1, new_letters 0, send_letters 0, found_flag 1, new_letters 1,
send_letters 1, merging_t 2, merge_t 2, merge, mergers 2, mergers 1, mergers 0, same_s 0, same_s 1, same_v 2, mean_t, mean_half, mean_v,
places_again 0, places_again 1, places_again 2, new_t 0, same_t 2, new_t 1, new_meanings, keep, send_meanings, spread_g 11 16, same_v 1, writers 2,
same_t 1, merged_again 2, writers 1, writers_places 2, merged_again 1, same_t 0, writers 0, writers_list 2, writers_places 1, merged_again 0, write 2,
writers_list 1, writers_places 0, write 1, writers_list 0, sums 1, change 2, write 0, sums 0, floors 1, more 1, rests 1, floors 0, sum_before 2,
rests 0, sum_before 3, spread_s 3 7, more 0, other 1, write_meanings 2, change 1, other 0, next 1 0, next 0 0, next 1 1, next 0 1, next 1 2, sums 2,
changes, spread_s 0 3, floors 2, spread_s 7 11, next 0 2, write_meanings 1, sums_v, next 1 3, more 2, rests 2, other 2, change 0, next 0 3"""


def rank_program(g, core, T, topo):
    rank = T.rank_of(core)
    if rank is None:
        return
    A, AF = AluOpType, ActivationFunctionType
    Q = {"v": g.vector, "s": g.scalar, "t": g.tensor, "g": g, "y": g.sync}
    own = {"v": "qv", "s": "qs", "t": "qt", "g": "qg"}
    cnt = {"v": 0, "s": 0, "t": 0, "g": 0}
    known = {q: {} for q in Q}
    past = {}
    acc = {}

    def ref(name, lo=0, hi=None, step=1, p=128):
        if name in SIDE:
            return ref("FL", SIDE[name] + lo, SIDE[name] + (K if hi is None else hi), step, p)
        hi = T[name].shape[1] if hi is None else hi
        return (name, lo, hi, T[name][0:p, lo:hi:step] if step != 1 else T[name][0:p, lo:hi], step)

    def meet(lo, hi, st, l2, h2, s2):
        return lo < h2 and l2 < hi and not (st == s2 and st > 1 and (lo - l2) % st)

    def is_ps(name):
        return name in SCRATCH and SCRATCH[name][0] == "psum"

    def need(q, reads, writes):
        me = own.get(q)
        dep = {}
        for rs, w in ((reads, False), (writes, True)):
            for (name, lo, hi, _, st) in rs:
                for (l2, h2, ev, c, w2, s2) in acc.get(name, []):
                    if is_ps(name):
                        hit = ev != me or (q != "t" and (w or w2) and l2 < hi and lo < h2)
                    else:
                        hit = (w or w2) and meet(lo, hi, st, l2, h2, s2)
                    if hit and dep.get(ev, 0) < c:
                        dep[ev] = c
        todo = {e: c for e, c in dep.items() if known[q].get(e, 0) < c}
        for e in list(todo):
            if any(f != e and past.get((f, todo[f]), {}).get(e, 0) >= todo[e] for f in todo):
                del todo[e]
        for e, c in todo.items():
            Q[q].wait_ge(T.sem[e], c)
            k = known[q]
            k[e] = max(k.get(e, 0), c)
            for e2, c2 in past.get((e, c), {}).items():
                k[e2] = max(k.get(e2, 0), c2)

    def note(ev, c, q, reads, writes):
        k = dict(known[q]) if q else {}
        k[ev] = c
        past[(ev, c)] = k
        for rs, w in ((reads, False), (writes, True)):
            for (name, lo, hi, _, st) in rs:
                old = acc.get(name, [])

                def inside(o):
                    return lo <= o[0] and o[1] <= hi and (st == 1 or (st == o[5] and (lo - o[0]) % st == 0))
                if w:
                    old = [o for o in old if not inside(o) or (is_ps(name) and o[2] != ev)]
                else:
                    old = [o for o in old if not (o[2] == ev and not o[4] and inside(o))]
                acc[name] = old + [(lo, hi, ev, c, w, st)]

    def do(q, fn, reads, writes):
        need(q, reads, writes)
        ins = fn()
        cnt[q] += 1
        ins.then_inc(T.sem[own[q]], 1)
        note(own[q], cnt[q], q, reads, writes)

    def rd(*xs):
        out = []
        for x in xs:
            if isinstance(x, tuple):
                out += x[1] if x[0] is None else [x]
        return out

    def ap(x):
        return x[3] if isinstance(x, tuple) else x

    def ind(win, off):
        return (None, [win, off], None, win[3].indirect(off[3]))

    def tt(out, a, b, op):
        do("v", lambda: g.vector.tensor_tensor(ap(out), ap(a), ap(b), op), rd(a, b), rd(out))

    def ts(out, a, s1, op0, s2=None, op1=None):
        if op1 is None:
            do("v", lambda: g.vector.tensor_scalar(ap(out), ap(a), ap(s1), None, op0), rd(a, s1), rd(out))
        else:
            do("v", lambda: g.vector.tensor_scalar(ap(out), ap(a), ap(s1), ap(s2), op0, op1), rd(a, s1, s2), rd(out))

    def cp(out, a):
        do("v", lambda: g.vector.tensor_copy(ap(out), ap(a)), rd(a), rd(out))

    def fill(out, c):
        do("v", lambda: g.vector.memset(ap(out), c), [], rd(out))

    def scan(out, a, b, op0, op1, first=0.0):
        do("v", lambda: g.vector.tensor_tensor_scan(ap(out), ap(a), ap(b), ap(first), op0, op1), rd(a, b, first), rd(out))

    def act(out, a, f, bias=0.0, scale=1.0, accum=None):
        if accum is None:
            do("s", lambda: g.scalar.activation(ap(out), ap(a), f, bias=ap(bias), scale=ap(scale)), rd(a, bias, scale), rd(out))
        else:
            do("s", lambda: g.scalar.activation(ap(out), ap(a), f, bias=ap(bias), scale=ap(scale), accum_out=ap(accum)), rd(a, bias, scale), rd(out, accum))

    def mm(out, l, r, start, stop):
        do("t", lambda: g.tensor.matmul(ap(out), ap(l), ap(r), start, stop), rd(l, r), rd(out))

    def group(out, terms, first=True, last=True):
        for j, (l, r) in enumerate(terms):
            mm(out, ref(l) if isinstance(l, str) else l, r, first and j == 0, last and j == len(terms) - 1)

    def iota(out, pattern, base, cm, small=True):
        if small:
            do("g", lambda: g.iota(ap(out), pattern, base, cm, allow_small_or_imprecise_dtypes=True), [], rd(out))
        else:
            do("g", lambda: g.iota(ap(out), pattern, base, cm), [], rd(out))

    def keep_where(out, a, pattern, op, other, cm, base=0):
        do("g", lambda: g.affine_select(ap(out), ap(a), pattern, op, other, base, cm), rd(a), rd(out))

    def load(q, out, src, sem):
        Q[q].dma_start(ap(out), src).then_inc(T.sem[sem], 16)
        note(sem, 16, None, [], rd(out))

    def store(q, dst, src, sem):
        need(q, rd(src), [])
        Q[q].dma_start(dst, ap(src)).then_inc(T.sem[sem], 16)
        note(sem, 16, q, rd(src), [])

    sent = [0]

    def send(src, dst, to, sem):
        c = T.cores[to]
        m = 0
        for e in topo.engines(core, c)[:NENG]:
            m |= 1 << e
        rid, pid, _ = topo.addr(c)
        need("g", rd(src), [])
        g.remote_dma(ap(dst), ap(src), T.sem[sem], T.sem["rl"], pid, rid, m)
        sent[0] += NENG

    lexw, mngw = ref("lx", K, K + W), ref("mn", K, K + W)

    load("y", ref("x0"), T.xw[:, :], "lx")
    load("y", ref("wti"), T.wts[:, :], "lw")
    load("s", lexw, T.lex[:, :], "ll")
    load("y", ref("m0"), T.gw[:, :], "lg")
    load("y", ref("thi"), T.th[:, :], "lt")
    load("s", mngw, T.mng[:, :], "lm")
    for t in (1, 2, 3):
        note("ax%d" % t, NENG, None, [], [ref("x%d" % t, 0, 2 * CH)])
        note("bx%d" % t, NENG, None, [], [ref("x%d" % t, 2 * CH, K)])
        note("ag%d" % t, NENG, None, [], [ref("m%d" % t)])

    def col(j):
        return ref("col", j, j + 1)
    PG, PL, PP, CF, THR, W1, W2, THA, THB, TH, BF8, BFX, BZ, C_WA, C_WB, THB0, NTHR = 0, 1, 2, 3, 4, 7, 8, 9, 10, 11, 12, 13, 14, 15, 16, 17, 18
    B, Id = ref("B"), ref("Id")
    BIG = 8192.0
    iota(ref("pi"), [[1, 1]], 0, 1, False)
    iota(ref("cq"), [[1, 128]], 0, 0)
    iota(ref("cg"), [[1, 8], [0, 16]], 0, 0)
    iota(ref("cl", 0, 16), [[1, 16]], 0, 0)
    ts(ref("pj", 0, 1), ref("pi"), 4, A.arith_shift_right)
    ts(ref("pj", 1, 2), ref("pi"), 15, A.bitwise_and)
    fill(ref("C6"), 6144.0)
    fill(ref("one"), 1.0)
    cp(col(PP), ref("pi"))
    cp(ref("col", PG, PG + 2), ref("pj", 0, 2))
    fill(ref("Z"), 0.0)
    ts(Id, ref("cq"), col(PP), A.is_equal)
    ts(B, ref("cg"), col(PG), A.is_equal)
    fill(ref("C7"), 191.0 * 1024)
    ts(ref("eq"), ref("cl", 0, 16), col(PL), A.is_equal)
    ts(col(CF), col(PL), -1.0, A.mult, 0.5, A.add)
    act(ref("NI4"), Id, AF.Copy, scale=-4096.0)
    act(ref("NI7"), Id, AF.Copy, scale=-131072.0)
    tt(ref("BmI"), B, Id, A.subtract)
    cp(ref("col", W1, W1 + 2), ref("wti"))
    ts(ref("cw"), ref("eq"), -17.0, A.mult, 1.0, A.add)
    cp(ref("B8"), ref("B", 0, 128, 16))
    ts(col(THB0), col(CF), -1.0, A.mult, 0.5, A.add)
    ts(ref("Wa"), ref("BmI"), col(W1), A.mult)
    ts(ref("Wb"), ref("BmI"), col(W2), A.mult)
    ts(ref("Wc"), ref("BmI"), col(W1), A.mult, 32.0, A.mult)
    ts(col(BF8), col(CF), BIG, A.mult, -8.0, A.add)
    ts(col(BFX), col(CF), 8 * BIG, A.mult, 64.0 - 8 * BIG, A.add)
    fill(ref("CK"), 0.0)
    for name, src, s in (("NB", "B", -1.0), ("W7", "B", -7 * BIG), ("NB8K", "B", -BIG), ("MI", "Id", -1.0), ("I8K", "Id", BIG)):
        act(ref(name), ref(src), AF.Copy, scale=s)
    keep_where(ref("L"), ref("NB"), [[1, 128]], A.is_gt, 0.0, -1)
    keep_where(ref("WF"), ref("L"), [[1, 128]], A.not_equal, 0.5, -1)

    def fallback(t):
        keep_where(ref("Wv%d" % t), ref("WF"), [[0, 128]], A.is_equal, 0.0, 0)
        keep_where(ref("G"), ref("WF", t, 128, 16), [[16, 8]], A.is_ge, -1.0 / 32, -1, t)
        keep_where(ref("Wv%d" % t, t, 128, 16), ref("G"), [[16, 8]], A.is_ge, 0.0, -1, 15)
    fallback(0)
    keep_where(ref("NL8K"), ref("NB8K"), [[1, 128]], A.is_gt, 0.0, -1)
    keep_where(ref("WL"), ref("W7"), [[1, 128]], A.not_equal, -8 * BIG, -1)
    iota(ref("i64"), [[1, 64]], 0, 0)
    iota(ref("ci"), [[16, 24]], -2048 - K, 0)
    iota(ref("sbi", p=64), [[0, 512]], 63, 1)
    iota(ref("rs0"), [[0, CH]], 0, 0)
    iota(ref("mk0", p=16), [[0, K]], 7 * 8192, 0)
    keep_where(ref("SEL", p=64), ref("sbi", p=64), [[-16, 4], [0, 8], [-1, 16]], A.is_equal, 0.0, 1)
    keep_where(ref("rs"), ref("rs0"), [[0, 8], [1, 16]], A.not_equal, -2.0 ** 31, 0)
    keep_where(ref("mk", p=16), ref("mk0", p=16), [[0, 24], [-1, 16]], A.is_equal, -2.0 ** 30, 1)
    keep_where(ref("mj", p=16), ref("rs0", p=16), [[0, 8], [-1, 16]], A.is_equal, -2.0 ** 30, 1)
    keep_where(ref("EQ", p=16), ref("one", p=16), [[0, 8], [-1, 16]], A.is_equal, 0.0, 1)
    fallback(1)
    fallback(2)

    def thresholds():
        ts(ref("pj", 2, 3), ref("thi"), 4, A.arith_shift_right)
        ts(ref("pj", 3, 4), ref("thi"), 15, A.bitwise_and)
        cp(col(TH), ref("thi"))
        cp(ref("col", THA, THA + 2), ref("pj", 2, 4))
        ts(col(BZ), col(TH), -0.5 - BIG, A.add)
        ts(col(C_WA), col(THA), 16.0 / BIG ** 2, A.mult, -4096.0 / BIG ** 2, A.add)
        ts(col(C_WB), col(THB), 1.0 / BIG ** 2, A.mult, -0.5 / BIG ** 2, A.add)
        ts(ref("cim"), ref("ci"), col(PL), A.add)
        ts(ref("WFA"), ref("B8"), col(C_WA), A.mult)
        ts(ref("WFB"), ref("B8"), col(C_WB), A.mult)
        for name, src, s in (("I64", "Id", 64.0), ("B8K", "B", BIG), ("NB128", "B", -128.0), ("B4K", "B", BIG / 2), ("NB4K", "B", -BIG / 2)):
            ts(ref(name), ref(src), s, A.mult)

    def constants_s():
        for t in range(VIS):
            act(col(THR + t), ref("eq", t, t + 1), AF.Identity, scale=-0.5 + (14 - t) / 32.0, bias=col(THB0))
        act(ref("WX"), ref("WF"), AF.Copy, scale=8 * BIG)
        for k in range(16):
            act(ref("CK", 129 * k, 128 * k + 128, 16), ref("B8"), AF.Copy, scale=ref("cw", k, k + 1))
        act(ref("col", NTHR, NTHR + VIS), ref("col", THR, THR + VIS), AF.Copy, scale=-1.0)

    def narrow():
        act(ref("Z", 15, 128, 16), ref("B8"), AF.Copy)
        for name, j, s in (("PP", 0, 0.5), ("PP", 8, 0.5), ("PM", 0, 0.5), ("PM", 8, -0.5), ("WFC", 0, 1.5), ("WFD", 0, -1.0 / BIG)):
            act(ref(name, j, j + 8), ref("B8"), AF.Copy, scale=s)

    def bk(b, lo=0, hi=K, p=128):
        return ref("b%d" % b, lo, hi, p=p)

    def blk(name, c):
        return ref(name, CH * c, CH * c + CH)

    def wrap(out, src, lo, hi):
        group(out, [(ref("Z", 15 - r, 143 - r), ref(src, lo + r, hi, 16)) for r in range(16)])

    HS, HU = (6, 2, 7), (3, 1, 5)

    def hash_sums(t, c):
        if t < VIS:
            xs = blk("x%d" % t, c)
            mm(bk(HS[c], 0, CH), ref("Wa"), xs, True, True)
            mm(bk(HS[c], CH, 2 * CH), ref("Wb"), xs, True, True)

    def hash_floors(t, c):
        if t < VIS:
            act(ref("Mh", 2 * CH * c, 2 * CH * (c + 1)), bk(HS[c], 0, 2 * CH), AF.Identity, bias=192.0 - 4095.0 / 8192.0, scale=1.0 / 4096.0)

    def hash_rests(t, c):
        if t < VIS:
            e, xs = 2 * CH * c, blk("x%d" % t, c)
            group(bk(HS[c], 2 * CH, 3 * CH), [("Wb", xs), ("NI4", ref("Mh", e + CH, e + 2 * CH))])
            group(bk(HU[c], 0, CH), [("C6", ref("one")), ("Wa", xs), ("NI4", ref("Mh", e, e + CH))])

    def hash_more(t, c):
        if t < VIS:
            group(bk(HU[c], CH, 2 * CH), [("C7", ref("one")), ("Wc", blk("x%d" % t, c)), ("NI7", ref("Mh", 2 * CH * c, 2 * CH * c + CH))])

    def hash_other(t, c):
        if t < VIS:
            act(blk("UP", c), bk(HS[c], 2 * CH, 3 * CH), AF.Identity, bias=786432.0)

    def hash_step(c, j):
        if j == 0:
            tt(blk("pr", c), blk("UP", c), bk(HU[c], 0, CH), A.mult)
        elif j == 1:
            tt(blk("pt", c), blk("pr", c), bk(HU[c], CH, 2 * CH), A.add)
        elif j == 2:
            ts(blk("hi", c), blk("pt", c), 5, A.arith_shift_right, 4095, A.bitwise_and)
        else:
            cp(blk("hu", c), blk("hi", c))

    def hash_next(t, c, j):
        if t + 1 < VIS:
            hash_step(c, j)

    def spread(t, q, ks):
        for k in ks if t < VIS else ():
            o, s = ref("X16", k, 16 * CH, 16), blk("x%d" % t, 0)
            if q == "v":
                cp(o, s)
            elif q == "g":
                keep_where(o, s, [[0, CH]], A.is_equal, 0.0, 0)
            else:
                act(o, s, AF.Copy)

    XBK, HFB, TAB, FREE = 4, 5, 4, (1, 5, 7)
    PART = ((0, 2 * CH), (2 * CH, K))
    AT = ({"count": (0, 0), "lowest": (1, 0), "place": (1, 256), "letter": (2, 0), "pair": (0, 0), "kept": (2, 0), "half": (0, 256), "far": (3, 0)},
          {"count": (6, 0), "lowest": (7, 0), "place": (7, 128), "letter": (6, 256), "pair": (6, 128), "kept": (6, 256), "half": (6, 384), "far": (6, 0)})

    def at(p, what, n=None, skip=0):
        b, c = AT[p][what]
        return bk(b, c + skip, c + skip + (PART[p][1] - PART[p][0] if n is None else n))

    def part(name, p, per=1):
        return ref(name, PART[p][0] // per, PART[p][1] // per)

    def look_v(i0, i1):
        tt(ref("D", 16 * i0, 16 * i1), ind(lexw, ref("hu", i0, i1)), ref("X16", 16 * i0, 16 * i1), A.not_equal)

    def look_s(i0, i1):
        act(ref("C", 16 * i0, 16 * i1), ind(lexw, ref("hu", i0, i1)), AF.Copy)

    def compare(i0, i1):
        for k in range(16):
            tt(ref("D", 16 * i0 + k, 16 * i1, 16), ref("C", 16 * i0 + k, 16 * i1, 16), bk(XBK, i0, i1), A.not_equal)

    def count(i0, i1):
        p = i0 // (2 * CH)
        group(at(p, "count", i1 - i0, i0 - PART[p][0]), [(ref("CK", 128 * k, 128 * k + 128), ref("D", 16 * i0 + k, 16 * i1, 16)) for k in range(16)])

    def pairs(p):
        act(part("pm", p), at(p, "count"), AF.Sign, bias=-13.5, scale=-1.0)

    def lowest(t, p):
        pm = part("pm", p)
        group(at(p, "lowest"), [("Wv%d" % t, pm)])
        group(at(p, "letter"), [("Id", part("x%d" % t, p)), ("WX", pm)])

    def pair_letter(p):
        act(part("Fx", p), at(p, "letter"), AF.Relu, bias=col(BFX))

    def pair_lane(p):
        act(part("Fm", p), at(p, "letter"), AF.Relu, bias=col(BF8), scale=0.125)

    def lane(t, c):
        ts(blk("Le", c), at(c // 2, "lowest", CH, CH * (c % 2)), col(THR + t), A.is_ge)

    def lane_s(t, half):
        if half == 0:
            act(part("RF", 0), at(0, "lowest"), AF.Sign, bias=col(NTHR + t))
        else:
            act(part("Le", 0), part("RF", 0), AF.Relu)

    def place(c):
        tt(blk("Lh", c), blk("Le", c), bk(HFB, CH * c, CH * c + CH), A.mult)

    def place_wrap(p):
        wrap(at(p, "place", (PART[p][1] - PART[p][0]) // 16), "Lh", *PART[p])

    def place_list(p):
        ts(part("le", p, 16), at(p, "place", (PART[p][1] - PART[p][0]) // 16), 2048.0, A.add)

    def letters(p):
        tt(part("LC", p), ind(lexw, part("le", p, 16)), part("Le", p), A.mult)

    def meanings(t, c):
        tt(blk("d", c), ind(mngw, ref("le", 8 * c, 8 * c + 8)), blk("m%d" % t, c), A.subtract)

    def distance(c):
        act(blk("ad", c), blk("d", c), AF.Abs)

    def blocks(p):
        return range(PART[p][0] // CH, PART[p][1] // CH)

    def halves_t(p):
        for j, c in enumerate(blocks(p)):
            group(at(p, "half", 16, 16 * j), [(blk("Fx", c), ref("PP")), (blk("LC", c), ref("PM"))])

    def halves_s(p):
        act(part("mr", p, 8), at(p, "half", 16 * len(blocks(p))), AF.Abs, bias=-32.0)

    def free_t(c):
        group(bk(FREE[c], 384, 392), [(blk("Le", c), ref("WFC")), (blk("Fm", c), ref("WFA")), (blk("Fm", c), ref("WFB")), (blk("ad", c), ref("WFD"))])

    def far_t(p):
        group(at(p, "far"), [("Id", part("Fm", p)), ("NB", part("ad", p))])

    def free_pair(p):
        act(part("Zf", p), at(p, "far"), AF.Sign, bias=col(BZ))

    def rows_s(c):
        for j in range(8):
            q = 8 * c + j
            act(ref("ab", 64 * q, 64 * q + 64), ref("i64"), AF.Abs, bias=ref("mr", 16 * c + j, 16 * c + j + 1), scale=-1.0)

    def rows_v(c):
        for j in range(8):
            q = 8 * c + j
            u = ref("U", 64 * q, 64 * q + 64)
            ts(u, ref("ab", 64 * q, 64 * q + 64), ref("mr", 16 * c + 8 + j, 16 * c + 9 + j), A.is_equal, bk(FREE[c], 384 + j, 385 + j), A.is_gt)

    def rows_t(c):
        for j in range(8):
            q = 8 * c + j
            u = ref("U", 64 * q, 64 * q + 64)
            mm(bk(TAB, 0, 64, p=64), u, u, q == 0, q == 23)

    def pair_t(p):
        group(at(p, "pair"), [("B", part("Fx", p))])

    def pair_s(p):
        act(part("Xf", p), at(p, "pair"), AF.Identity, bias=-1.0)

    def kept_t(t, p):
        group(at(p, "kept"), [("Id", part("x%d" % t, p)), ("I8K", part("Le", p)), ("MI", part("Fm", p))])

    def kept_s(p):
        act(part("xp", p), at(p, "kept"), AF.Copy)

    WB, Z1, MB, HB, DB, GB, ZB = (0, 6), 5, 2, 3, 7, 4, (0, 3, 1)
    pw, lfw, again = bk(2, 256, 304), bk(1, 272, 296), bk(2, 384, 512)

    def table_rows():
        for b in range(4):
            mm(bk(TAB, 64 + 64 * b, 128 + 64 * b), ref("SEL", 128 * b, 128 * b + 128, p=64), ref("TS", p=64), True, True)

    def found_t(p):
        group(bk(WB[p], *PART[p]), [("Id", part("LC", p)), ("WL", part("Le", p)), ("B", part("Fm", p))], True, False)

    def flagged(p):
        tt(part("RF", p), ind(ref("TW"), part("lf", p, 16)), part("Xf", p), A.is_equal)

    def new_letters(xn, p):
        tt(part(xn, p), part("xp", p), bk(WB[p], *PART[p]), A.min)

    def zb(c, lo=0, hi=CH):
        return bk(ZB[c], lo, hi)

    def ends(name, c):
        return ref(name, CH * c + 15, CH * c + CH, 16)

    def listed(name, c):
        return ref(name, 8 * c, 8 * c + 8)

    def row(q, lo, hi):
        return ("E", CH * q + lo, CH * q + hi, T["E"][:, q, lo:hi], 1)

    def same_v(c):
        for q in range(8 * c, 8 * c + 8):
            i0, i1 = 16 * q, CH * (c + 1)
            ts(row(q, 0, i1 - i0), ref("Hb", i0, i1), ref("s1", i0 + 15, i0 + 16), A.is_equal)

    def same_s(half):
        for q in range(8):
            apart = ref("ab", CH * q, CH * q + CH - 16 * q)
            if half == 0:
                act(apart, bk(2, 384 + 16 * q, 512), AF.Abs, bias=ref("s1", 16 * q + 15, 16 * q + 16), scale=-1.0)
            else:
                act(row(q, 0, CH - 16 * q), apart, AF.Relu, bias=1.0, scale=-1.0)

    def same_t(c):
        for j in range(7):
            mm(zb(c, 16 * j + 16), ref("NB8K"), row(8 * c + j, 16, CH - 16 * j), False, False)
        mm(zb(c), ref("NL8K"), ("E", 8 * CH * c, 8 * CH * (c + 1), T["E"][:, 8 * c:8 * c + 8, 0:16], 1), False, True)

    def scatter(buf, src, c):
        w, o, s = ref(buf), listed("lo", c), blk(src, c)
        do("v", lambda: g.vector.tensor_copy(w[3].indirect(o[3]), s[3]), [o, s], [w])

    spread(0, "v", range(16))
    for c in (1, 0, 2):
        hash_sums(0, c)
        hash_floors(0, c)
    for c in (1, 0, 2):
        hash_rests(0, c)
        hash_more(0, c)
        hash_other(0, c)
    constants_s()
    for j in range(4):
        for c in (1, 0):
            hash_step(c, j)
    for t in range(VIS):
        x, m, last, u = "x%d" % t, "m%d" % t, t == VIS - 1, t + 1
        xn, gn = "xn%d" % t, "gn%d" % t
        to = (rank + 2) % N if last else (rank - 1) % N

        step = {
            "hash": hash_step, "look_v": look_v, "look_s": look_s, "compare": compare, "count": count,
            "words_t": lambda: mm(bk(XBK, CH, K), Id, ref(x, CH, K), True, True),
            "places_v": lambda: ts(ref("hf"), ref("hu"), -2048.0, A.add),
            "places_t": lambda: mm(bk(HFB), Id, ref("hf"), True, True),
            "pairs": pairs, "lowest": lambda p: lowest(t, p), "pair_letter": pair_letter, "pair_lane": pair_lane,
            "lane": lambda c: lane(t, c), "lane_s": lambda h: lane_s(t, h), "narrow": lambda: t == 0 and narrow(),
            "place": place, "place_wrap": place_wrap, "place_list": place_list,
            "old_meanings": lambda c: scatter("mn", "gn%d" % (t - 1), c) if t > 0 else (c == 0 and thresholds()),
            "letters": letters, "pair_t": pair_t, "pair_s": pair_s, "kept_t": lambda p: kept_t(t, p), "kept_s": kept_s,
            "meanings": lambda c: meanings(t, c), "distance": distance, "free_t": free_t, "far_t": far_t, "not_free": free_pair,
            "halves_t": halves_t, "halves_s": halves_s, "rows_s": rows_s, "rows_v": rows_v, "rows_t": rows_t,
            "table": lambda: ts(ref("TS", p=64), bk(TAB, 0, 64, p=64), 1.0, A.min), "table_t": table_rows,
            "table_v": lambda: cp(ref("TW"), bk(TAB, 64, 320)), "code_wrap": lambda: wrap(pw, "FL", 0, 2 * K),
            "own_high": lambda: act(ref("XB"), bk(2, 256, 280), AF.Identity, bias=128.0 - 15.0 / 32, scale=1.0 / 16),
            "code_low": lambda: act(ref("CB"), bk(2, 280, 304), AF.Copy), "code_high": lambda: group(lfw, [("Id", ref("CB")), ("I64", ref("XB"))]),
            "code_list": lambda: ts(ref("lf"), lfw, -64.0 * 132, A.add), "flagged": flagged,
            "found_t": found_t, "found_far": lambda p: mm(bk(WB[p], *PART[p]), ref("NB4K"), part("Zf", p), False, False),
            "found_flag": lambda p: mm(bk(WB[p], *PART[p]), ref("B8K"), part("RF", p), False, True),
            "new_letters": lambda p: new_letters(xn, p), "send_letters": lambda p: send(part(xn, p), part("x%d" % u, p), to, "%sx%d" % ("ab"[p], u)),
            "merge_t": lambda j: mm(bk(MB), ref(("B4K", "NB8K")[j - 1]), ref(("Zf", "RF")[j - 1]), j == 1, j == 2),
            "merge": lambda: act(ref("M"), bk(MB), AF.Relu, scale=1.0 / BIG, bias=8.0),
            "half": lambda: act(ref("ha"), ref("ad"), AF.Identity, bias=127.8, scale=0.5),
            "below": lambda: act(ref("nd"), ref("d"), AF.Relu, scale=-1.0),
            "mean_t": lambda: group(bk(DB), [("NB128", ref("Le")), ("MI", ref("nd"))], True, False),
            "mean_half": lambda: mm(bk(DB), Id, ref("ha"), False, True), "mean_v": lambda: tt(ref("gd"), ref("M"), bk(DB), A.mult),
            "new_t": lambda j: mm(bk(GB), Id, ref((m, "gd")[j]), j == 0, j == 1), "new_meanings": lambda: act(ref(gn), bk(GB), AF.Copy),
            "send_meanings": lambda: send(ref(gn), ref("m%d" % u), to, "ag%d" % u),
            "all_t": lambda: mm(bk(HB, CH, K), B, ref("Lh", CH, K), True, True), "all_v": lambda c: cp(blk("Hb", c), bk(HB, CH * c, CH * c + CH)),
            "again_t": lambda: mm(again, B, blk("Lh", 0), True, True),
            "masked_t": lambda: group(bk(Z1), [(ref("EQ", p=16), ref("mk", p=16)), ("B", ref("Lh"))], True, False),
            "merging_t": lambda j: mm(bk(Z1), ref(("B4K", "NB8K")[j - 1]), ref(("Zf", "RF")[j - 1]), False, j == 2),
            "mergers": lambda c: scan(blk("s1", c), ref("rs"), bk(Z1, CH * c, CH * c + CH), A.add, A.max),
            "places_again": lambda c: mm(zb(c), ref("EQ", p=16), ref("mj", p=16), True, False),
            "same_v": same_v, "same_s": same_s, "same_t": same_t,
            "writers": lambda c: scan(blk("sj", c), ref("rs"), zb(c), A.add, A.max),
            "merged_again": lambda c: tt(listed("zz", c), ends("sj", c), ends("s1", c), A.add),
            "writers_places": lambda c: tt(listed("z", c), listed("zz", c), listed("cim", c), A.max),
            "writers_list": lambda c: ts(listed("lo", c), listed("z", c), 2048.0 + K, A.add), "write": lambda c: scatter("lx", xn, c),
            "sum_before": lambda j: last and act(ref("C", 1024 * j, 1024 * j + 1024), ref("mn", K + 1024 * j, K + 1024 * j + 1024), AF.Copy,
                                                 accum=ref("ya", j, j + 1)),
            "keep": lambda: last and act(ref("mn", 0, K), bk(GB), AF.Copy),
            "change": lambda c: last and tt(blk("df", c), ind(ref("mn"), listed("lo", c)), blk(gn, c), A.subtract),
            "write_meanings": lambda c: (last or c == 2) and scatter("mn", gn, c),
            "changes": lambda: last and act(ref("D", 0, 2 * CH), ref("df", CH, K), AF.Copy, scale=-1.0, accum=ref("ya", 4, 5)),
            "sums_v": lambda: last and do("v", lambda: g.vector.tensor_reduce(ref("yb")[3], ref("ya")[3], AxisListType.X, A.add), [ref("ya")], [ref("yb")]),
            "sums": lambda c: hash_sums(u, c), "floors": lambda c: hash_floors(u, c), "rests": lambda c: hash_rests(u, c), "other": lambda c: hash_other(u, c),
            "more": lambda c: hash_more(u, c),
            "next": lambda c, j: hash_next(t, c, j), "spread_s": lambda a, b: spread(u, "s", range(a, b)), "spread_g": lambda a, b: spread(u, "g", range(a, b)),
        }
        for call in ORDER.replace("\n", " ").split(","):
            name, *args = call.split()
            step[name](*[int(a) for a in args])

    store("y", T.yl[:, :], lexw, "ol")
    store("y", T.yx[:, :], ref("x3"), "ox")
    store("y", T.yg[:, :], ref("m3"), "og")
    scan(blk("sj", 0), ref("one"), blk("df", 0), A.mult, A.subtract, ref("yb"))
    store("s", T.ym[:, :], ref("sj", CH - 1, CH), "om")
    for q in ("v", "s", "t", "g"):
        g.wait_ge(T.sem[own[q]], cnt[q])
    g.wait_ge(T.sem["rl"], sent[0])
    for s in ("ox", "og", "ol", "om"):
        g.wait_ge(T.sem[s], 16)
